import numpy as np, ml_dtypes
CORES = [40,41,42,43,44,45,46,47]
N = 8
import mx_ref
BF = ml_dtypes.bfloat16
def gcols(t, e):
    v = np.concatenate([t.reshape(8, 16, -1, 4), np.zeros((8, 16, 1, 4), BF)], axis=2)
    return np.ascontiguousarray(np.stack([v[g][:, e[g]] for g in range(8)])).reshape(128, -1)
def tile(rs):
    return np.stack(rs, axis=2).reshape(128, -1).astype(BF)
def cut(t, i, w=512):
    return t[:, w * i:w * i + w]
def pick(q, e):
    c = np.concatenate([q[0].reshape(128, -1, 4), np.zeros((128, 1, 4), np.uint8)], axis=1); s = np.concatenate([q[1], np.ones((16, 1), np.uint8)], axis=1)
    return (np.ascontiguousarray(c[:, e].reshape(128, -1)), np.ascontiguousarray(s[:, e]))
def join(*qs):
    return (np.concatenate([q[0] for q in qs], axis=1), np.concatenate([q[1] for q in qs], axis=1))
def put(q, e, v):
    c, s = q[0].reshape(128, -1, 4).copy(), q[1].copy(); c[:, e] = v[0].reshape(128, -1, 4); s[:, e] = v[1]
    return (c.reshape(128, -1), s)
def pk(c, s):
    return (np.ascontiguousarray(c), mx_ref.live(s))
def emit(q):
    return q[0], q[1]
def packed(v, rng):
    q = [mx_ref.quantize(np.ascontiguousarray(v[r])) for r in range(N)]
    return np.stack([a for a, b in q]), np.stack([mx_ref.plane(b, rng) for a, b in q])
def values_of_codes():
    e, c = np.zeros((128, 128, 4), np.float32), np.zeros((128, 2, 4), np.uint8)
    e[np.arange(128), np.arange(128), 0] = 1
    c[:127, :, 0] = np.arange(256).reshape(2, 128).T[:127]
    return mx_ref.matmul(mx_ref.quantize(e.reshape(128, 512).astype(BF)), (c.reshape(128, 8), np.full((16, 2), 127, np.uint8))).T.reshape(-1).astype(np.float64)
CODE_VALUE, SCALE_VALUE = values_of_codes(), 2.0 ** (np.arange(256) - 127.0)
def decode(q):
    return (CODE_VALUE[q[0]].reshape(16, 8, -1, 4) * SCALE_VALUE[q[1]][:, None, :, None] + 0.0).reshape(128, -1).astype(np.float32)
def f(rng, *shape):
    return mx_ref.flush((rng.standard_normal(shape, dtype=np.float32) * np.exp2(rng.integers(-2, 3, shape[:-1] + (1,)))).astype(BF))
def wide(rng, *shape, cols=0):
    v = rng.standard_normal(shape, dtype=np.float32) * np.exp2(rng.integers(-12, 13, shape)).astype(np.float32)
    if cols: v *= np.repeat(np.exp2(rng.integers(-cols, cols + 1, shape[:-2] + (1, shape[-1] // 4))) * (rng.random(shape[:-2] + (1, shape[-1] // 4)) > 0.0625), 4, axis=-1).astype(np.float32)
    return mx_ref.flush(v.astype(BF))
C, S, R = 448, 128, 2
STEP = [1, 2]
def partner(r, t):
    return r ^ STEP[t]
def order(p):
    return np.argsort(-(p[::16] + np.float32(0.0)), axis=1, kind="stable")
def walk(pi):
    g, p = np.arange(8), np.zeros(8, int)
    e, taken = np.zeros((8, C), int), np.zeros((8, C), bool)
    for k in range(C):
        e[:, k] = p
        taken[g, p] = True
        p = pi[g, p]
        p = np.where(taken[g, p], np.argmin(taken, axis=1), p)
    return e
def common(w, rng):
    c, p = packed(np.stack([w] * N), rng)
    return {"wc": c, "ws": p}
def weights(rng, keep=()):
    w = np.array(f(rng, 128, 2048)).reshape(128, 4, 8, 16, 4)
    for p in keep: w[:, :, :, p] = 0
    if len(keep): w[::16] = 0
    return common(w.reshape(128, 2048), rng)
def numbers_of(rng):
    return {"x": np.array(f(rng, N, 128, 4 * C)), "u": np.stack([f(rng, 128, 512)] * N), "v": np.array(f(rng, N, 128, 512))}
def planted(rng, s, sign, kind):
    d = numbers_of(rng)
    x = d["x"].astype(np.float32).reshape(N, 8, 16, C, 4)
    digit = ((s[:, :, :, None] >> np.arange(12)) & 1) * np.exp2(np.arange(12) - 23.0)
    x[:, :, 0] = 0
    x[:, :, 0, :, 0] = sign[:, :, None]
    for a in range(3): x[:, :, 8 + a] = digit[:, :, :, 4 * a:4 * a + 4]
    x[:, :, 11:] = rng.integers(4, 8, (N, 8, 5, C, 4)) * rng.choice([-1.0, 1.0], (N, 8, 5, C, 4)) * 2.0 ** -20
    u = d["u"].reshape(N, 128, 128, 4)
    u[:, :, ::16] = 0
    for g in range(8):
        k = 1.0 if kind[g] < 2 else 2.0 ** -30
        u[:, 16 * g, 16 * g, 0] = k
        u[:, 16 * g + 8:16 * g + 11, 16 * g] = k
        if kind[g] == 1: x[:, g, 0, int(rng.integers(C)), 0] *= 2.0 ** 30
        if kind[g] == 3:
            x[:, g, 0] = 0
            x[:, g, 8:] *= 2.0 ** -7
            x[:, g, 8:11] *= sign[:, g][:, None, None, None]
            x[:, g, 11] = 0
            u[:, 16 * g + 11, 16 * g, 0] = 1.125 * k
            u[:, 16 * g + 11, 16 * g, 1] = k
            for r in range(N):
                if r & STEP[0]:
                    j = int(np.flatnonzero(s[r, g] == 0)[-1])
                    x[r, g, 11, j, 0] = 1.125 * 2.0 ** -30
                    x[r, g, 11, j, 1] = -1.25 * 2.0 ** -30
    return {"x": x.reshape(N, 128, 4 * C).astype(BF), "u": u.reshape(N, 128, 512), "v": d["v"], **weights(rng, [0] + [*range(8, 16)])}
def setup_inputs(rng):
    return {**numbers_of(rng), **weights(rng)}
def setup_inputs_ties(rng):
    d = numbers_of(rng)
    e = rng.permutation(N)
    x = d["x"].reshape(N, 8, 16, C, 4)
    for r in range(N):
        for g in range(8):
            k = np.zeros(C, int) if r == e[0] else rng.permutation(C) % 3
            a = x[r, g, :8, :3].copy()
            a[:, 2] = 0
            x[r, g, :8] = a[:, k]
    x[e[1]] = 0
    u = d["u"].reshape(N, 8, 16, 128, 4)
    for g in range(8):
        own = u[:, g, :8, 16 * g].copy()
        u[:, :, :, 16 * g] = 0
        u[:, g, :8, 16 * g] = own
    return {"x": x.reshape(N, 128, 4 * C), "u": u.reshape(N, 128, 512), "v": d["v"], **weights(rng, [*range(8)])}
def setup_inputs_near(rng):
    s = np.stack([np.stack([rng.permutation(C) // 2 for g in range(8)]) for r in range(N)])
    sign = np.stack([rng.permutation(8) % 2 * 2.0 - 1.0 for r in range(N)])
    return planted(rng, s, sign, rng.permutation(8) % 4)
def setup_inputs_cycles(rng):
    size = [[C], [257] + [1] * (C - 257), [2] * (C // 2), [3] * (C // 3) + [1] * (C % 3)]
    s = np.zeros((N, 8, C), int)
    h = rng.permutation(8)
    for q in range(N):
        if q & (STEP[0] | STEP[1]): continue
        for g in range(8):
            i, m, pi, at = rng.permutation(C), rng.permutation(C), np.zeros(C, int), 0
            if h[g] // 2 == 0:
                m = np.roll(m, -int(np.argmin(m)))
                m[1:3] = np.sort(m[1:3])
                m[-2:] = np.sort(m[-2:])[::-1]
            for n in size[h[g] // 2]:
                pi[m[at:at + n]] = np.roll(m[at:at + n], -1)
                at += n
            other = i.copy()
            if h[g] == 4:
                k = pi[np.flatnonzero(pi > np.arange(C))[-2:]]
                other[k] = i[k[::-1]]
            for r in (q, q ^ STEP[0], q ^ STEP[1], q ^ STEP[0] ^ STEP[1]):
                c = other if r & STEP[1] else i
                s[r, g] = C - 1 - (c[pi] if r & STEP[h[g] % 2] else c)
    sign = np.tile(rng.permutation(8) % 2 * 2.0 - 1.0, (N, 1))
    return planted(rng, s, sign, rng.permutation(8) % 2 * 2)
def setup_inputs_huge(rng):
    d = numbers_of(rng)
    x = 2.0 ** 30 * (0.9 + 0.1 * rng.random((N, 128, C, 4)))
    x[:, ::8, :, 0] = 2.0 ** 30
    c = np.stack([rng.permutation(C) % 2 * 2.0 - 1.0 for r in range(N)])
    c[rng.permutation(N) < N // 2] = 1
    x *= c[:, None, :, None]
    u = d["u"].reshape(N, 128, 128, 4)
    a = 2.0 ** 30 * (1 - 0.1 * rng.random((128, 8, 4))) * (rng.permutation(8) % 2 * 2.0 - 1.0)[None, :, None]
    u[:, :, ::16] = a.astype(np.float32).astype(BF)
    w = np.zeros((128, 4, 128, 4), np.float32)
    i = np.arange(128)
    for b in range(4): w[i, b, i, b] = -8
    return {"x": x.astype(np.float32).reshape(N, 128, 4 * C).astype(BF), "u": u.reshape(N, 128, 512), "v": d["v"], **common(w.reshape(128, 2048).astype(BF), rng)}
def setup_inputs_spread(rng):
    d = setup_inputs(rng)
    d["x"] = wide(rng, N, 128, 4 * C, cols=6)
    return d
def check_inputs(d):
    b = []
    for k in ("x", "u", "v"):
        a = np.abs(d[k].astype(np.float32))
        if not (np.isfinite(a).all() and ((a == 0) | (a >= 2.0 ** -30) & (a <= 2.0 ** 30)).all()): b.append("a value of " + k)
    if (d["u"].astype(np.float32) != d["u"][:1].astype(np.float32)).any(): b.append("u differs between ranks")
    if (d["wc"] % 128 == 127).any(): b.append("a code of wc is no number")
    if (d["wc"] != d["wc"][:1]).any(): b.append("wc differs between ranks")
    s = [mx_ref.live(p) for p in d["ws"]]
    if any((p != s[0]).any() for p in s): b.append("ws differs between ranks")
    return b
def reference(x, u, v, wc, ws):
    w, qu = pk(wc[0], ws[0]), mx_ref.quantize(u[0])
    now = [x[r] for r in range(N)]
    for t in range(R):
        o = [order(mx_ref.matmul(qu, mx_ref.quantize(now[r]))) for r in range(N)]
        i = [np.argsort(o[r], axis=1) for r in range(N)]
        e = [walk(np.take_along_axis(o[r], i[partner(r, t)], axis=1)) for r in range(N)]
        laid = [gcols(now[r], e[r]) for r in range(N)]
        came = decode(join(*[mx_ref.quantize(np.ascontiguousarray(laid[r][:, :4 * S])) for r in range(N)])).astype(BF)
        for r in range(N):
            z = np.ascontiguousarray(np.concatenate([cut(came, partner(r, t), 4 * S), laid[r][:, 4 * S:]], axis=1))
            q = mx_ref.quantize(z)
            now[r] = tile([z[:, b::4].astype(np.float32) + mx_ref.matmul(pick(w, np.arange(128 * b, 128 * b + 128)), q) * np.float32(0.015625) for b in range(4)])
    y, el = np.zeros((N, 128, C), np.float32), np.zeros((N, 8, C), np.float32)
    oc, osc = np.zeros((N, 128, 4 * C), np.uint8), np.zeros((N, 16, C), np.uint8)
    for r in range(N):
        q = mx_ref.quantize(now[r])
        y[r] = mx_ref.matmul(mx_ref.quantize(v[r]), q)
        el[r] = e[r]
        oc[r], osc[r] = emit(q)
    return {"y": y, "el": el, "oc": oc, "osc": osc}

@@ -1,0 +1,381 @@
+from concourse.mybir import dt, AluOpType as A, ActivationFunctionType as F
+
+C, S, R = 448, 128, 2
+STEP = [1, 2]
+KB = C // 16
+HALF = 6
+SLOT = 16 * HALF
+MID = KB - 2 * HALF
+EARLY = MID - 5
+ENGINES = 8
+H2, H1 = (0, S), (S, C)
+MAGIC = 12582912.0
+DROP, HOLD = -8192.0, 1024.0
+
+SCRATCH = {}
+
+
+def _buf(dtype, n, *names):
+    for name in names:
+        SCRATCH[name] = ("psum" if name[:2] in ("pp", "pr") and name[2:].isdigit() else "sbuf", [128, n], dtype)
+
+
+_buf("bfloat16", 512, "ub", "vb", "one", "bt0", "bt1")
+_buf("bfloat16", 4 * 512, "eb")
+_buf("bfloat16", C, "gateb", "eqr", "eqs", *["%s%d" % (n, i) for n in ("bit", "rel", "junk") for i in range(4)])
+_buf("bfloat16", SLOT * HALF, "sgate", "shb", "shs")
+_buf("bfloat16", 224 * MID, "zs")
+_buf("bfloat16", 4 * C, "z64", "x0", "x1", "x2", "zt0", "zt1")
+_buf("float8_e4m3fn_x4", 128, "qu", "qur", "qv", "qb0", "qb1", "qc0", "qc1")
+_buf("uint8", 128, "su", "sur", "sv", "sb0", "sb1", "sc0", "sc1")
+_buf("float8_e4m3fn_x4", 512, "qw", "qe")
+_buf("uint8", 512, "sw", "se")
+_buf("float8_e4m3fn_x4", C, "qx0", "qx1", "qx2", "qz0", "qz1")
+_buf("uint8", C, "sx0", "sx1", "sx2", "sz0", "sz1")
+_buf("int32", C, "ci", "d15")
+_buf("int32", 8, "ku")
+_buf("int32", KB, "kl")
+_buf("int32", 2, "pc")
+_buf("uint16", 8, "offu")
+_buf("uint16", KB, "offl", "offm", "offp", "off0", "off1", "own0", "own1", "land0", "land1", "offe0", "offe1", "offe2", "offe3")
+_buf("float32", C, "mask", "gate", "ctl", "ct1", "ct2", "f0", "fh", "f15", "f25", "mrow", "arow", "srow", "orow", "hrow",
+     "wrow", "crow", "prow", "erow", "ysb", "j0", "j1", "a0", "a1", "b0", "b1", "r0", "r1", "r2", "r3")
+_buf("float32", 8, "hold", "colj", "colm", "cole")
+_buf("float32", KB, "k0", "cnt", "tc", "pl")
+_buf("float32", 32, "aw", "an")
+_buf("float32", 512, "pp0", "pp1", "pp2", "pp3", "pr0", "pr1", "pr2", "pr3")
+
+LOADS = ["ldu", "ldx1", "ldx2", "ldw", "ldv"]
+SEMAPHORES = ["cv", "cs", "ct", "cg", "stored", "sent", "rxi0", "rxi1", "rxb0", "rxb1"] + LOADS
+
+
+def rank_program(g, core, T, topo):
+    rank = T.rank_of(core)
+    if rank is None:
+        return
+    queue = {"v": g.vector, "s": g.scalar, "t": g.tensor, "g": g, "y": g.sync}
+    count = {}
+    know = {q: {} for q in queue}
+    writer, reader = {}, {}
+
+    def wait(q, tok):
+        _, sem, val, seen = tok
+        if know[q].get(sem, 0) >= val:
+            return
+        queue[q].wait_ge(T.sem[sem], val)
+        for s, n in list(seen.items()) + [(sem, val)]:
+            know[q][s] = max(know[q].get(s, 0), n)
+
+    def before(q, reads, writes):
+        for k in reads:
+            for tok in writer.get(k, []):
+                wait(q, tok)
+            if k[:2] in ("pp", "pr"):
+                for tok in reader.get(k, []):
+                    if tok[0] != q:
+                        wait(q, tok)
+        for k in writes:
+            for tok in writer.get(k, []) + reader.get(k, []):
+                wait(q, tok)
+
+    def after(q, sem, inc, reads, writes):
+        count[sem] = count.get(sem, 0) + inc
+        tok = (q, sem, count[sem], dict(know[q]))
+        for k in reads:
+            reader.setdefault(k, []).append(tok)
+        for k in writes:
+            writer[k], reader[k] = [tok], []
+
+    def do(q, reads, writes, make):
+        before(q, reads, writes)
+        make(queue[q]).then_inc(T.sem["c" + q], 1)
+        after(q, "c" + q, 1, reads, writes)
+
+    def load(q, sem, total, key, out, in_):
+        queue[q].dma_start(out, in_).then_inc(T.sem[sem], 16)
+        count[sem] = count.get(sem, 0) + 16
+        writer.setdefault(key, []).append((q, sem, total, {}))
+
+    def store(q, reads, out, in_):
+        before(q, reads, [])
+        queue[q].dma_start(out, in_).then_inc(T.sem["stored"], 16)
+        after(q, "stored", 16, reads, [])
+
+    def send(t, pairs, sem):
+        dst = T.cores[rank ^ STEP[t]]
+        rid, pid, _ = topo.addr(dst)
+        eng = topo.engines(core, dst)[:ENGINES]
+        mask = sum(1 << e for e in eng)
+        total = count.get(sem, 0) + len(pairs) * len(eng)
+        for there, here, view, key in pairs:
+            before("g", [key], [])
+            g.remote_dma(view(there), view(here), T.sem[sem], T.sem["sent"], pid, rid, mask)
+            count["sent"] = count.get("sent", 0) + len(eng)
+            writer[there] = [("far", sem, total, {})]
+        count[sem] = total
+
+    def ts(out, in0, s1, op0, s2=None, op1=None):
+        if op1 is None:
+            return lambda e: e.tensor_scalar(out, in0, s1, None, op0)
+        return lambda e: e.tensor_scalar(out, in0, s1, s2, op0, op1)
+
+    def tt(out, in0, in1, op):
+        return lambda e: e.tensor_tensor(out, in0, in1, op)
+
+    def act(out, in_, func=F.Copy, **kw):
+        return lambda e: e.activation(out, in_, func, **kw)
+
+    def cp(out, in_):
+        return lambda e: e.tensor_copy(out, in_)
+
+    def fill(out, x):
+        return lambda e: e.memset(out, x)
+
+    def quant(q, s, x):
+        return lambda e: e.quantize_mx(q, s, x)
+
+    def scan(out, d0, d1, init, op0, op1):
+        return lambda e: e.tensor_tensor_scan(out, d0, d1, init, op0, op1)
+
+    def iota(name, pattern, base, cm, **kw):
+        do("g", [], [name], lambda e: e.iota(T[name][:], pattern, base, cm, **kw))
+
+    load("s", "ldu", 16, "ub", T.ub[:], T.u[:])
+    load("y", "ldx1", 16, "x0:1", T.x0[:, 4 * S:4 * C], T.x[:, 4 * S:4 * C])
+    load("y", "ldx2", 16, "x0:2", T.x0[:, 0:4 * S], T.x[:, 0:4 * S])
+    load("s", "ldw", 32, "w", T.qw[:].bitcast(dt.uint8), T.wc[:])
+    load("s", "ldw", 32, "w", T.sw[:], T.ws[:])
+    load("y", "ldv", 16, "vb", T.vb[:], T.v[:])
+
+    number = {"allow_small_or_imprecise_dtypes": True}
+    iota("ku", [[16, 8]], 0, 0)
+    iota("ci", [[-1, C]], C, 1)
+    iota("kl", [[1, KB]], 0, 0)
+    iota("pc", [[0, 2]], 0, 1)
+    iota("k0", [[16, KB]], 16, 0, **number)
+    iota("f0", [[1, C]], 0, 0, **number)
+    do("v", [], ["one"], fill(T.one[:], 1.0))
+    do("v", ["ku"], ["offu"], cp(T.offu[:], T.ku[:]))
+    do("v", ["ci"], ["d15"], ts(T.d15[:], T.ci[:], 15, A.bitwise_and))
+    do("v", [], ["sgate"], fill(T.sgate[:], 1.0))
+    do("v", ["d15"], ["mask"], ts(T.mask[:], T.d15[:], 0, A.is_equal))
+    do("v", ["sgate"], ["sgate"], fill(T.sgate[:, 0:SLOT * HALF:SLOT], 0.0))
+    do("v", ["d15"], ["gate"], ts(T.gate[:], T.d15[:], 0, A.not_equal))
+    do("v", ["sgate"], ["sgate"], fill(T.sgate[:, 16:SLOT * HALF:SLOT + 16], 0.0))
+    do("v", ["ub"], ["qu"], quant(T.qu[:], T.su[:], T.ub[:]))
+    do("v", ["kl"], ["offl"], cp(T.offl[:], T.kl[:]))
+    do("v", ["qu", "offu"], ["qur"], cp(T.qur[:, 0:128].bitcast(dt.uint32), T.qu[:, 0:128].bitcast(dt.uint32).indirect(T.offu[:, 0:8])))
+    do("v", ["qu", "offu"], ["sur"], cp(T.sur[:, 0:128], T.su[:, 0:128].indirect(T.offu[:, 0:8])))
+    do("v", ["d15"], ["gateb"], ts(T.gateb[:], T.d15[:], 0, A.not_equal))
+    do("v", ["k0"], ["k0"], fill(T.k0[:, 0:HALF], 0.0))
+    do("v", ["k0"], ["k0"], fill(T.k0[:, HALF:KB - HALF], 224.0))
+    for b in range(4):
+        do("g", ["one"], ["eb%d" % b], lambda e: e.affine_select(
+            T.eb[:, 512 * b:512 * b + 512], T.one[:], [[-1, 512]], A.is_equal, 0.0, b, 4))
+    for name, off in (("fh", -0.5), ("f15", -1.5), ("f25", -2.5)):
+        do("s", ["f0"], [name], act(T[name][:], T.f0[:], F.Identity, bias=off))
+
+    def later_constants():
+        do("v", ["d15"], ["ct1"], ts(T.ct1[:], T.d15[:], 15, A.is_equal, HOLD, A.mult))
+        do("v", ["d15"], ["ct2"], ts(T.ct2[:], T.d15[:], 0, A.is_equal, DROP, A.mult))
+        do("v", ["pc"], ["pc"], ts(T.pc[:], T.pc[:], 15, A.bitwise_and))
+        do("v", ["ct1", "ct2"], ["ctl"], tt(T.ctl[:], T.ct1[:], T.ct2[:], A.add))
+        do("v", ["pc"], ["hold"], ts(T.hold[:, 0:1], T.pc[:, 0:1], 15, A.is_lt, -HOLD, A.mult))
+        do("v", ["hold"], ["colj"], ts(T.colj[:, 0:1], T.hold[:, 0:1], 0.5, A.add))
+        do("v", ["hold"], ["colm"], ts(T.colm[:, 0:1], T.hold[:, 0:1], MAGIC + 1.0, A.add))
+        for i in range(4):
+            do("v", ["hold"], ["cole%d" % i], ts(T.cole[:, i:i + 1], T.hold[:, 0:1], 0.25 * i, A.add))
+        do("v", ["eb%d" % b for b in range(4)], ["qe"], quant(T.qe[:], T.se[:], T.eb[:]))
+        do("v", ["vb"], ["qv"], quant(T.qv[:], T.sv[:], T.vb[:]))
+
+    def matmul(out, key, lhs, ls, lkey, rhs, rs, rkey):
+        do("t", lkey + rkey, [key], lambda e: e.matmul_mx(out, lhs, ls, rhs, rs, True, True))
+
+    def state_keys(t, h):
+        return ["x0:%d" % h] if t == 0 else ["x%d:%d:%d" % (t, h, i) for i in range(4)]
+
+    def quant_state(t, h, part):
+        a, b = part
+        do("v", state_keys(t, h), ["qx%d:%d" % (t, h)], quant(T["qx%d" % t][:, a:b], T["sx%d" % t][:, a:b], T["x%d" % t][:, 4 * a:4 * b]))
+
+    def score(t, h, part):
+        a, b = part
+        p0, p1 = ("pp0", "pp1") if h == 1 else ("pp2", "pp3")
+        qx, sx = T["qx%d" % t], T["sx%d" % t]
+        for p in (p0, p1):
+            matmul(T[p][:, 0:b - a], p, T.qur[:], T.sur[:], ["qur", "sur"], qx[:, a:b], sx[:, a:b], ["qx%d:%d" % (t, h)])
+        do("v", [p0, "mask"], ["mrow:%d" % h], tt(T.mrow[:, a:b], T[p0][:, 0:b - a], T.mask[:, a:b], A.mult))
+        do("s", [p1], ["srow:%d" % h], act(T.srow[:, a:b], T[p1][:, 0:b - a]))
+        do("v", ["mrow:%d" % h, "gate"], ["arow:%d" % h], scan(T.arow[:, a:b], T.gate[:, a:b], T.mrow[:, a:b], 0.0, A.mult, A.add))
+
+    def settle(t, a, b):
+        counts = ["cntm"] if b == KB else []
+        counts += ["cnt%d" % k for k in range(a, b) if k < HALF or k >= KB - HALF]
+        key = "own%d:%d" % (t, a)
+        do("v", ["tc"] + counts, ["pl:%d" % a], tt(T.pl[:, a:b], T.cnt[:, a:b], T.tc[:, a:b], A.add))
+        do("v", ["pl:%d" % a], [key], cp(T["own%d" % t][:, a:b], T.pl[:, a:b]))
+        send(t, [("land%d" % t, "own%d" % t, lambda n: T[n][:, a:b], key)], "rxi%d" % t)
+
+    def places(t):
+        do("v", ["arow:1", "arow:2"], ["aw"], cp(T.aw[:, 0:KB], T.arow[:, 15:C:16]))
+        do("v", ["arow:1", "arow:2"], ["an"], ts(T.an[:, 0:KB], T.arow[:, 15:C:16], -1.0, A.mult))
+        row = ["srow:1", "srow:2"]
+        pend = []
+
+        def sign(k, i, a, b, sgn):
+            do("s", ["rel%d" % i], ["cnt%d" % k, "junk%d" % i],
+               act(T["junk%d" % i][:, a:b], T["rel%d" % i][:, a:b], F.Sign, scale=sgn, accum_out=T.cnt[:, k:k + 1]))
+
+        for n in range(2 * HALF):
+            k, i = n if n < HALF else KB - 2 * HALF + n, n % 4
+            if k < HALF:
+                a, b, sgn, key, col = 16 * k + 16, C, 1.0, "an", T.an
+            else:
+                a, b, sgn, key, col = 0, 16 * k + 16, -1.0, "aw", T.aw
+            do("s", row + [key], ["rel%d" % i], act(T["rel%d" % i][:, a:b], T.srow[:, a:b], F.Relu, bias=col[:, k:k + 1], scale=sgn))
+            pend.append((k, i, a, b, sgn))
+            if n:
+                sign(*pend.pop(0))
+        sign(*pend.pop(0))
+        do("v", ["aw", "offl"] + row, ["eqr"], tt(T.eqr[:], T.aw[:, 0:KB].indirect(T.offl[:, 0:KB]), T.srow[:], A.is_equal))
+        shk = []
+        for i in range(HALF):
+            a, n, k = SLOT * i, 16 * (i + 1), KB - HALF + i
+            do("v", row + ["aw"], ["shb:%d" % i], ts(T.shb[:, a:a + n], T.srow[:, 0:n], T.aw[:, i:i + 1], A.is_ge))
+            shk.append("shb:%d" % i)
+            if k < KB - 1:
+                do("v", row + ["aw"], ["shb:h%d" % i], ts(T.shb[:, a + n:a + SLOT], T.srow[:, 16 * k + 16:C], T.aw[:, k:k + 1], A.is_gt))
+                shk.append("shb:h%d" % i)
+        do("v", ["eqr", "gateb"], ["eqs"], scan(T.eqs[:], T.gateb[:], T.eqr[:], 0.0, A.mult, A.add))
+        late = [
+            lambda: do("v", shk + ["sgate"], ["shs"], scan(T.shs[:], T.sgate[:], T.shb[:], 0.0, A.mult, A.add)),
+            lambda: do("v", ["eqs", "k0"], ["tc"], tt(T.tc[:], T.k0[:], T.eqs[:, 15:C:16], A.subtract)),
+            lambda: do("v", ["tc", "shs"], ["tc"], tt(T.tc[:, 0:HALF], T.tc[:, 0:HALF], T.shs[:, 15:SLOT * HALF:SLOT + 16], A.add)),
+            lambda: do("v", ["tc", "shs"], ["tc"], tt(T.tc[:, KB - HALF:KB - 1], T.tc[:, KB - HALF:KB - 1],
+                                                      T.shs[:, SLOT - 1:SLOT * (HALF - 1):SLOT], A.add)),
+        ]
+
+        def add_up(i):
+            bit = "bit%d" % (i % 4)
+            do("v", [bit + "l", bit + "r"], ["zs:%d" % i], scan(T.zs[:, 224 * i:224 * i + 224], T[bit][:, 0:224], T[bit][:, 224:C], -224.0, A.add, A.add))
+
+        for i in range(MID):
+            k = HALF + i
+            m, bit = 16 * k + 16, "bit%d" % (i % 4)
+            do("v", row + ["aw"], [bit + "l"], ts(T[bit][:, 0:m], T.srow[:, 0:m], T.aw[:, k:k + 1], A.is_ge))
+            do("v", row + ["aw"], [bit + "r"], ts(T[bit][:, m:C], T.srow[:, m:C], T.aw[:, k:k + 1], A.is_gt))
+            if i > 0:
+                add_up(i - 1)
+            if late:
+                late.pop(0)()
+            if t == 0 and i == EARLY:
+                settle(t, 0, HALF)
+        add_up(MID - 1)
+        do("v", ["zs:%d" % i for i in range(MID)], ["cntm"], cp(T.cnt[:, HALF:KB - HALF], T.zs[:, 223:224 * MID:224]))
+        settle(t, HALF if t == 0 else 0, KB)
+
+    def wrap(row, key):
+        do("v", [key, "ctl"], ["hrow"], scan(T.hrow[:], T.ctl[:], row, 0.0, A.add, A.max))
+        return T.hrow[:, 15:C:16]
+
+    def cycles(t):
+        own, land = "own%d" % t, "land%d" % t
+        do("v", [own + ":0", own + ":%d" % HALF, "fh"], ["orow"], cp(T.orow[:, 0:C].indirect(T[own][:, 0:KB]), T.fh[:]))
+        if t == 0:
+            later_constants()
+        do("s", ["orow", land], ["j0"], act(T.j0[:], T.orow[:, 0:C].indirect(T[land][:, 0:KB])))
+        do("s", ["j0"], ["b0"], act(T.b0[:], T.j0[:], F.Identity, bias=-1.0 / 512))
+        h = wrap(T.j0[:], "j0")
+        do("v", ["hrow", "colj"], ["off0"], ts(T.off0[:], h, T.colj[:, 0:1], A.add))
+        win, wkey = T.j0, "j0"
+        for k in range(9):
+            off, j, jn = "off%d" % (k % 2), "j%d" % (k % 2), "j%d" % ((k + 1) % 2)
+            an, bk, bn = "a%d" % (k % 2), "b%d" % (k % 2), "b%d" % ((k + 1) % 2)
+            if k < 8:
+                do("s", [j, off], [jn], act(T[jn][:], T[j][:, 0:C].indirect(T[off][:, 0:KB])))
+            do("v", [wkey, off, bk], [an], tt(T[an][:], win[:, 0:C].indirect(T[off][:, 0:KB]), T[bk][:], A.min))
+            win, wkey = T[an], an
+            if k < 8:
+                do("s", [an], [bn], act(T[bn][:], T[an][:], F.Identity, bias=-(2.0 ** (k + 1)) / 512))
+                h = wrap(T[jn][:], jn)
+                o = "off%d" % ((k + 1) % 2)
+                do("v", ["hrow", "colj"], [o], ts(T[o][:], h, T.colj[:, 0:1], A.add))
+        h = wrap(win[:], wkey)
+        do("v", [wkey, "f15"], ["wrow"], scan(T.wrow[:], win[:], T.f15[:], -4.0, A.max, A.max))
+        do("v", ["hrow", "colm"], ["offm"], ts(T.offm[:], h, T.colm[:, 0:1], A.add, MAGIC, A.subtract))
+        do("v", ["wrow", "f25"], ["crow"], scan(T.crow[:], T.wrow[:], T.f25[:], -2.5, A.add, A.subtract))
+        do("v", ["crow", "offm", wkey], ["prow"], tt(T.prow[:], T.crow[:, 0:C].indirect(T.offm[:, 0:KB]), win[:], A.subtract))
+        h = wrap(T.prow[:], "prow")
+        do("v", ["hrow", "hold"], ["offp"], ts(T.offp[:], h, T.hold[:, 0:1], A.add, 512.0, A.mult))
+        do("v", ["offp", "f0"], ["erow"], cp(T.erow[:, 0:C].indirect(T.offp[:, 0:KB]), T.f0[:]))
+        h = wrap(T.erow[:], "erow")
+        for i in (2, 0, 3, 1):
+            do("v", ["hrow", "cole%d" % i], ["offe%d" % i], ts(T["offe%d" % i][:], h, T.cole[:, i:i + 1], A.add, 4.0, A.mult))
+
+    def lay_out(t, tile, key, part):
+        a, b = part
+        for i in (2, 0, 3, 1):
+            out = tile[:, 4 * a + i:4 * b:4]
+            src = T["x%d" % t][:, 0:4 * C].indirect(T["offe%d" % i][:, a // 16:b // 16])
+            do("v" if i < 2 else "s", state_keys(t, 1) + state_keys(t, 2) + ["offe%d" % i], [key + str(i)], cp(out, src) if i < 2 else act(out, src))
+
+    def products(t, h, part):
+        a, b = part
+        zt, qz, sz = T["zt%d" % t], T["qz%d" % t], T["sz%d" % t]
+        zk = ["z%d:%d:%d" % (t, h, i) for i in range(4)]
+        do("v", zk, ["qz%d:%d" % (t, h)], quant(qz[:, a:b], sz[:, a:b], zt[:, 4 * a:4 * b]))
+        if h == 1:
+            do("v", zk, ["z64:%d" % h], ts(T.z64[:, 4 * a:4 * b], zt[:, 4 * a:4 * b], 64.0, A.mult))
+        else:
+            do("s", zk, ["z64:%d" % h], act(T.z64[:, 4 * a:4 * b], zt[:, 4 * a:4 * b], scale=64.0))
+        for i in range(4):
+            matmul(T["pr%d" % i][:, 0:b - a], "pr%d" % i, T.qw[:, S * i:S * i + S], T.sw[:, S * i:S * i + S], ["w"],
+                   qz[:, a:b], sz[:, a:b], ["qz%d:%d" % (t, h)])
+
+    def sums(t, h, part):
+        a, b = part
+        for i in range(4):
+            do("v", ["pr%d" % i, "z64:%d" % h], ["r%d:%d" % (i, h)],
+               tt(T["r%d" % i][:, a:b], T["pr%d" % i][:, 0:b - a], T.z64[:, 4 * a + i:4 * b:4], A.add))
+            do("s", ["r%d:%d" % (i, h)], ["x%d:%d:%d" % (t + 1, h, i)],
+               act(T["x%d" % (t + 1)][:, 4 * a + i:4 * b:4], T["r%d" % i][:, a:b], scale=0.015625))
+
+    def finish(t, h, part):
+        a, b = part
+        q, s, key, p = T["qx%d" % t], T["sx%d" % t], "qx%d:%d" % (t, h), "pp0" if h == 1 else "pp2"
+        store("y", [key], T.oc[:, 4 * a:4 * b], q[:, a:b].bitcast(dt.uint8))
+        matmul(T[p][:, 0:b - a], p, T.qv[:], T.sv[:], ["qv"], q[:, a:b], s[:, a:b], [key])
+        do("s", [p], ["ysb:%d" % h], act(T.ysb[:, a:b], T[p][:, 0:b - a]))
+        for k in range(4):
+            store("y", [key], T.osc[4 * k:4 * k + 4, a:b], s[32 * k:32 * k + 4, a:b])
+        store("s", ["ysb:%d" % h], T.y[:, a:b], T.ysb[:, a:b])
+
+    quant_state(0, 1, H1)
+    score(0, 1, H1)
+    quant_state(0, 2, H2)
+    score(0, 2, H2)
+    for t in range(R):
+        places(t)
+        cycles(t)
+        if t == R - 1:
+            store("y", ["erow"], T.el[:], T.erow[0:128:16, :])
+        bt, qb, sb, qc, sc = ["%s%d" % (n, t) for n in ("bt", "qb", "sb", "qc", "sc")]
+        lay_out(t, T[bt], bt + ":", H2)
+        do("v", [bt + ":%d" % i for i in range(4)], [qb, sb], quant(T[qb][:], T[sb][:], T[bt][:]))
+        send(t, [(qc, qb, lambda n: T[n][:].bitcast(dt.uint8), qb), (sc, sb, lambda n: T[n][:], sb)], "rxb%d" % t)
+        lay_out(t, T["zt%d" % t], "z%d:1:" % t, H1)
+        products(t, 1, H1)
+        sums(t, 1, H1)
+        for i in (2, 0, 3, 1):
+            matmul(T["pr%d" % i][:, 0:S], "pr%d" % i, T.qe[:, S * i:S * i + S], T.se[:, S * i:S * i + S], ["qe"], T[qc][:], T[sc][:], [qc, sc])
+            out, src = T["zt%d" % t][:, i:4 * S:4], T["pr%d" % i][:, 0:S]
+            do("v" if i < 2 else "s", ["pr%d" % i], ["z%d:2:%d" % (t, i)], cp(out, src) if i < 2 else act(out, src))
+        products(t, 2, H2)
+        quant_state(t + 1, 1, H1)
+        sums(t, 2, H2)
+        last = score if t < R - 1 else finish
+        last(t + 1, 1, H1)
+        quant_state(t + 1, 2, H2)
+        last(t + 1, 2, H2)
+    for sem in sorted(count):
+        g.wait_ge(T.sem[sem], count[sem])

@@ -3,14 +3,16 @@ from concourse.mybir import dt, AluOpType as A, ActivationFunctionType as F
 C, S, R = 448, 128, 2
 STEP = [1, 2]
 KB = C // 16
-HALF = 6
-SLOT = 16 * HALF
-MID = KB - 2 * HALF
-EARLY = MID - 5
+NQ = KB // 4
+WIDE = [max(128, 64 * (i + 1)) for i in range(NQ)]
+AT = [sum(WIDE[:i]) for i in range(NQ + 1)]
+FROM_S = 20
+FIRST = 24
+PLAN = [*range(19, 7, -1), "q6", 7, 6, 5, 4, "early", "q4", "q3", "q2", 3, 2, 1, 0, "q1", "tally", "q0", "q5"]
 ENGINES = 8
 H2, H1 = (0, S), (S, C)
-MAGIC = 12582912.0
-DROP, HOLD = -8192.0, 1024.0
+MAGIC = 12582912
+LIFT, DROP = 512, 8192
 
 SCRATCH = {}
 
@@ -20,29 +22,31 @@ def _buf(dtype, n, *names):
         SCRATCH[name] = ("psum" if name[:2] in ("pp", "pr") and name[2:].isdigit() else "sbuf", [128, n], dtype)
 
 
-_buf("bfloat16", 512, "ub", "vb", "one", "bt0", "bt1")
+_buf("bfloat16", 512, "ub", "vb", "one", "go", "gs", "bt0", "bt1")
 _buf("bfloat16", 4 * 512, "eb")
-_buf("bfloat16", C, "gateb", "eqr", "eqs", *["%s%d" % (n, i) for n in ("bit", "rel", "junk") for i in range(4)])
-_buf("bfloat16", SLOT * HALF, "sgate", "shb", "shs")
-_buf("bfloat16", 224 * MID, "zs")
+_buf("bfloat16", C, "gatee", "eqr", "eqs", "rel0", "rel1", "rel2", "rel3")
+_buf("bfloat16", 224 * FROM_S, "zs")
 _buf("bfloat16", 4 * C, "z64", "x0", "x1", "x2", "zt0", "zt1")
-_buf("float8_e4m3fn_x4", 128, "qu", "qur", "qv", "qb0", "qb1", "qc0", "qc1")
-_buf("uint8", 128, "su", "sur", "sv", "sb0", "sb1", "sc0", "sc1")
+_buf("float8_e4m3fn_x4", 128, "qu", "qur", "qv", "qg", "qb0", "qb1", "qc0", "qc1")
+_buf("uint8", 128, "su", "sur", "sv", "sg", "sb0", "sb1", "sc0", "sc1")
 _buf("float8_e4m3fn_x4", 512, "qw", "qe")
 _buf("uint8", 512, "sw", "se")
 _buf("float8_e4m3fn_x4", C, "qx0", "qx1", "qx2", "qz0", "qz1")
 _buf("uint8", C, "sx0", "sx1", "sx2", "sz0", "sz1")
+_buf("bfloat16", 4 * AT[NQ], "fl")
+_buf("float8_e4m3fn_x4", AT[NQ], "qf")
+_buf("uint8", AT[NQ], "sf")
 _buf("int32", C, "ci", "d15")
 _buf("int32", 8, "ku")
 _buf("int32", KB, "kl")
 _buf("int32", 2, "pc")
 _buf("uint16", 8, "offu")
 _buf("uint16", KB, "offl", "offm", "offp", "off0", "off1", "own0", "own1", "land0", "land1", "offe0", "offe1", "offe2", "offe3")
-_buf("float32", C, "mask", "gate", "ctl", "ct1", "ct2", "f0", "fh", "f15", "f25", "mrow", "arow", "srow", "orow", "hrow",
+_buf("float32", C, "mask", "gate", "ctl", "f0", "fh", "f15", "f25", "mrow", "arow", "srow", "orow", "hrow", "hcol",
      "wrow", "crow", "prow", "erow", "ysb", "j0", "j1", "a0", "a1", "b0", "b1", "r0", "r1", "r2", "r3")
 _buf("float32", 8, "hold", "colj", "colm", "cole")
-_buf("float32", KB, "k0", "cnt", "tc", "pl")
-_buf("float32", 32, "aw", "an")
+_buf("float32", KB, "k0", "cnt", "tie", "base", "pl")
+_buf("float32", 32, "aw")
 _buf("float32", 512, "pp0", "pp1", "pp2", "pp3", "pr0", "pr1", "pr2", "pr3")
 
 LOADS = ["ldu", "ldx1", "ldx2", "ldw", "ldv"]
@@ -137,59 +141,65 @@ def rank_program(g, core, T, topo):
     def scan(out, d0, d1, init, op0, op1):
         return lambda e: e.tensor_tensor_scan(out, d0, d1, init, op0, op1)
 
-    def iota(name, pattern, base, cm, **kw):
-        do("g", [], [name], lambda e: e.iota(T[name][:], pattern, base, cm, **kw))
+    def iota(name, pattern, base, cm, cols=slice(None), key=None):
+        kw = {} if SCRATCH[name][2] == "int32" else {"allow_small_or_imprecise_dtypes": True}
+        do("g", [], [key or name], lambda e: e.iota(T[name][:, cols], pattern, base, cm, **kw))
 
     load("s", "ldu", 16, "ub", T.ub[:], T.u[:])
     load("y", "ldx1", 16, "x0:1", T.x0[:, 4 * S:4 * C], T.x[:, 4 * S:4 * C])
     load("y", "ldx2", 16, "x0:2", T.x0[:, 0:4 * S], T.x[:, 0:4 * S])
-    load("s", "ldw", 32, "w", T.qw[:].bitcast(dt.uint8), T.wc[:])
-    load("s", "ldw", 32, "w", T.sw[:], T.ws[:])
+    before("y", ["x0:1", "x0:2"], [])
+    load("y", "ldw", 32, "w", T.qw[:].bitcast(dt.uint8), T.wc[:])
+    load("y", "ldw", 32, "w", T.sw[:], T.ws[:])
     load("y", "ldv", 16, "vb", T.vb[:], T.v[:])
 
-    number = {"allow_small_or_imprecise_dtypes": True}
     iota("ku", [[16, 8]], 0, 0)
     iota("ci", [[-1, C]], C, 1)
     iota("kl", [[1, KB]], 0, 0)
     iota("pc", [[0, 2]], 0, 1)
-    iota("k0", [[16, KB]], 16, 0, **number)
-    iota("f0", [[1, C]], 0, 0, **number)
+    iota("f0", [[1, C]], 0, 0)
+    low = C - 16 * (KB - FROM_S)
+    iota("k0", [[0, 1]], low - MAGIC, 0, slice(0, 1), "k0:0")
+    iota("k0", [[-16, FROM_S - 1]], low + 224 - 16 - MAGIC, 0, slice(1, FROM_S), "k0:v")
+    iota("k0", [[16, KB - FROM_S]], 16 * FROM_S - MAGIC, 0, slice(FROM_S, KB), "k0:s")
     do("v", [], ["one"], fill(T.one[:], 1.0))
     do("v", ["ku"], ["offu"], cp(T.offu[:], T.ku[:]))
     do("v", ["ci"], ["d15"], ts(T.d15[:], T.ci[:], 15, A.bitwise_and))
-    do("v", [], ["sgate"], fill(T.sgate[:], 1.0))
+    do("v", [], ["cnt0"], fill(T.cnt[:, 0:1], 0.0))
     do("v", ["d15"], ["mask"], ts(T.mask[:], T.d15[:], 0, A.is_equal))
-    do("v", ["sgate"], ["sgate"], fill(T.sgate[:, 0:SLOT * HALF:SLOT], 0.0))
     do("v", ["d15"], ["gate"], ts(T.gate[:], T.d15[:], 0, A.not_equal))
-    do("v", ["sgate"], ["sgate"], fill(T.sgate[:, 16:SLOT * HALF:SLOT + 16], 0.0))
     do("v", ["ub"], ["qu"], quant(T.qu[:], T.su[:], T.ub[:]))
     do("v", ["kl"], ["offl"], cp(T.offl[:], T.kl[:]))
     do("v", ["qu", "offu"], ["qur"], cp(T.qur[:, 0:128].bitcast(dt.uint32), T.qu[:, 0:128].bitcast(dt.uint32).indirect(T.offu[:, 0:8])))
     do("v", ["qu", "offu"], ["sur"], cp(T.sur[:, 0:128], T.su[:, 0:128].indirect(T.offu[:, 0:8])))
-    do("v", ["d15"], ["gateb"], ts(T.gateb[:], T.d15[:], 0, A.not_equal))
-    do("v", ["k0"], ["k0"], fill(T.k0[:, 0:HALF], 0.0))
-    do("v", ["k0"], ["k0"], fill(T.k0[:, HALF:KB - HALF], 224.0))
+    do("v", ["pc"], ["pc"], ts(T.pc[:], T.pc[:], 15, A.bitwise_and))
+    do("v", ["mask"], ["gatee"], ts(T.gatee[:], T.mask[:], 63.0, A.mult, 1.0, A.add))
+    do("v", ["mask"], ["ctl"], ts(T.ctl[:], T.mask[:], -float(LIFT + DROP), A.mult, float(LIFT), A.add))
+    do("v", ["gatee"], ["gatee"], fill(T.gatee[:, 0:C:16], 0.0))
+    do("v", ["pc"], ["hold"], ts(T.hold[:, 0:1], T.pc[:, 0:1], LIFT, A.mult, -15 * LIFT, A.add))
+    do("g", ["one"], ["go"], lambda e: e.affine_select(T.go[:], T.one[:], [[-16, 8], [0, 64]], A.is_ge, 0.0, 0, 1))
+    do("g", ["go"], ["gs"], lambda e: e.affine_select(T.gs[:], T.go[:], [[16, 8], [0, 64]], A.is_ge, 0.0, 15, -1))
     for b in range(4):
         do("g", ["one"], ["eb%d" % b], lambda e: e.affine_select(
             T.eb[:, 512 * b:512 * b + 512], T.one[:], [[-1, 512]], A.is_equal, 0.0, b, 4))
+    for i in range(NQ):
+        for j in range(64 * i, WIDE[i], 64):
+            z = 4 * (AT[i] + j)
+            do("s", ["f0"], ["fl%d" % k for k in range(4 * i, 4 * i + 4)] if j == 64 * i else ["flz%d" % i],
+               act(T.fl[:, z:z + 256], T.f0[:, 0:256], scale=0.0))
     for name, off in (("fh", -0.5), ("f15", -1.5), ("f25", -2.5)):
         do("s", ["f0"], [name], act(T[name][:], T.f0[:], F.Identity, bias=off))
 
     def later_constants():
-        do("v", ["d15"], ["ct1"], ts(T.ct1[:], T.d15[:], 15, A.is_equal, HOLD, A.mult))
-        do("v", ["d15"], ["ct2"], ts(T.ct2[:], T.d15[:], 0, A.is_equal, DROP, A.mult))
-        do("v", ["pc"], ["pc"], ts(T.pc[:], T.pc[:], 15, A.bitwise_and))
-        do("v", ["ct1", "ct2"], ["ctl"], tt(T.ctl[:], T.ct1[:], T.ct2[:], A.add))
-        do("v", ["pc"], ["hold"], ts(T.hold[:, 0:1], T.pc[:, 0:1], 15, A.is_lt, -HOLD, A.mult))
         do("v", ["hold"], ["colj"], ts(T.colj[:, 0:1], T.hold[:, 0:1], 0.5, A.add))
-        do("v", ["hold"], ["colm"], ts(T.colm[:, 0:1], T.hold[:, 0:1], MAGIC + 1.0, A.add))
+        do("v", ["hold"], ["colm"], ts(T.colm[:, 0:1], T.hold[:, 0:1], float(MAGIC + 1), A.add))
         for i in range(4):
             do("v", ["hold"], ["cole%d" % i], ts(T.cole[:, i:i + 1], T.hold[:, 0:1], 0.25 * i, A.add))
         do("v", ["eb%d" % b for b in range(4)], ["qe"], quant(T.qe[:], T.se[:], T.eb[:]))
         do("v", ["vb"], ["qv"], quant(T.qv[:], T.sv[:], T.vb[:]))
 
-    def matmul(out, key, lhs, ls, lkey, rhs, rs, rkey):
-        do("t", lkey + rkey, [key], lambda e: e.matmul_mx(out, lhs, ls, rhs, rs, True, True))
+    def matmul(out, key, lhs, ls, lkey, rhs, rs, rkey, start=True, stop=True):
+        do("t", lkey + rkey, [key], lambda e: e.matmul_mx(out, lhs, ls, rhs, rs, start, stop))
 
     def state_keys(t, h):
         return ["x0:%d" % h] if t == 0 else ["x%d:%d:%d" % (t, h, i) for i in range(4)]
@@ -200,79 +210,92 @@ def rank_program(g, core, T, topo):
 
     def score(t, h, part):
         a, b = part
-        p0, p1 = ("pp0", "pp1") if h == 1 else ("pp2", "pp3")
         qx, sx = T["qx%d" % t], T["sx%d" % t]
-        for p in (p0, p1):
+        for p in ("pp0", "pp1") if h == 1 else ("pp2", "pp3"):
             matmul(T[p][:, 0:b - a], p, T.qur[:], T.sur[:], ["qur", "sur"], qx[:, a:b], sx[:, a:b], ["qx%d:%d" % (t, h)])
+
+    def take_scores(t, h, part):
+        a, b = part
+        p0, p1 = ("pp0", "pp1") if h == 1 else ("pp2", "pp3")
         do("v", [p0, "mask"], ["mrow:%d" % h], tt(T.mrow[:, a:b], T[p0][:, 0:b - a], T.mask[:, a:b], A.mult))
         do("s", [p1], ["srow:%d" % h], act(T.srow[:, a:b], T[p1][:, 0:b - a]))
         do("v", ["mrow:%d" % h, "gate"], ["arow:%d" % h], scan(T.arow[:, a:b], T.gate[:, a:b], T.mrow[:, a:b], 0.0, A.mult, A.add))
 
-    def settle(t, a, b):
-        counts = ["cntm"] if b == KB else []
-        counts += ["cnt%d" % k for k in range(a, b) if k < HALF or k >= KB - HALF]
+    def add_base(a, b, keys):
+        do("v", keys + ["cnt%d" % k for k in range(max(a, FROM_S), b)] + ["tie", "cnt0"], ["base:%d" % a],
+           tt(T.base[:, a:b], T.cnt[:, a:b], T.tie[:, a:b], A.add))
+
+    def settle(t, bank, a, b):
+        do("v", [bank, "ctl"], ["hcol:%d" % a], scan(T.hcol[:, 16 * a:16 * b], T.ctl[:, 16 * a:16 * b], T[bank][:, 16 * a:16 * b], 0.0, A.add, A.max))
+        do("v", ["hcol:%d" % a, "base:%d" % a], ["pl:%d" % a], tt(T.pl[:, a:b], T.base[:, a:b], T.hcol[:, 16 * a + 15:16 * b:16], A.subtract))
         key = "own%d:%d" % (t, a)
-        do("v", ["tc"] + counts, ["pl:%d" % a], tt(T.pl[:, a:b], T.cnt[:, a:b], T.tc[:, a:b], A.add))
-        do("v", ["pl:%d" % a], [key], cp(T["own%d" % t][:, a:b], T.pl[:, a:b]))
+        do("v", ["pl:%d" % a, "hold"], [key], ts(T["own%d" % t][:, a:b], T.pl[:, a:b], T.hold[:, 0:1], A.subtract))
         send(t, [("land%d" % t, "own%d" % t, lambda n: T[n][:, a:b], key)], "rxi%d" % t)
 
     def places(t):
-        do("v", ["arow:1", "arow:2"], ["aw"], cp(T.aw[:, 0:KB], T.arow[:, 15:C:16]))
-        do("v", ["arow:1", "arow:2"], ["an"], ts(T.an[:, 0:KB], T.arow[:, 15:C:16], -1.0, A.mult))
         row = ["srow:1", "srow:2"]
-        pend = []
+        do("v", ["arow:1", "arow:2"], ["aw"], cp(T.aw[:, 0:KB], T.arow[:, 15:C:16]))
+        pend, done = [], []
 
-        def sign(k, i, a, b, sgn):
-            do("s", ["rel%d" % i], ["cnt%d" % k, "junk%d" % i],
-               act(T["junk%d" % i][:, a:b], T["rel%d" % i][:, a:b], F.Sign, scale=sgn, accum_out=T.cnt[:, k:k + 1]))
+        def flags(k, a, b):
+            z = 4 * AT[k // 4]
+            return T.fl[:, z + 4 * a + k % 4:z + 4 * b:4]
 
-        for n in range(2 * HALF):
-            k, i = n if n < HALF else KB - 2 * HALF + n, n % 4
-            if k < HALF:
-                a, b, sgn, key, col = 16 * k + 16, C, 1.0, "an", T.an
+        def sign(k):
+            rel = "rel%d" % (k % 4)
+            do("s", [rel], ["fl%d" % k, "cnt%d" % k], act(flags(k, 0, 16 * k), T[rel][:, 0:16 * k], F.Sign, scale=-1.0, accum_out=T.cnt[:, k:k + 1]))
+            do("s", [rel], ["fld%d" % k], act(flags(k, 16 * k, 16 * k + 16), T[rel][:, 16 * k:16 * k + 16], F.Sign, scale=-1.0))
+
+        for k in range(KB - 1, FROM_S - 1, -1):
+            rel = "rel%d" % (k % 4)
+            do("s", row + ["aw"], [rel], act(T[rel][:, 0:16 * k + 16], T.srow[:, 0:16 * k + 16], F.Relu, bias=T.aw[:, k:k + 1], scale=-1.0))
+            pend.append(k)
+            if len(pend) > 1:
+                sign(pend.pop(0))
+        sign(pend.pop(0))
+
+        def add_up(k):
+            z = 224 * k + 224
+            do("v", ["fl%d" % k], ["zs:%d" % k], scan(T.zs[:, z - 8 * k:z], flags(k, 0, 8 * k), flags(k, 8 * k, 16 * k), -224.0, A.add, A.add))
+
+        def sum_up(i):
+            a, b = AT[i], AT[i + 1]
+            keys = [n % k for k in range(4 * i, 4 * i + 4) for n in ("fl%d", "fld%d")] + ["flz%d" % i]
+            do("v", keys, ["qf%d" % i], quant(T.qf[:, a:b], T.sf[:, a:b], T.fl[:, 4 * a:4 * b]))
+            side = (T.qg[:], T.sg[:], ["qg"], T.qf[:, a:b], T.sf[:, a:b], ["qf%d" % i])
+            if t == 0 and i == NQ - 1:
+                matmul(T.pp0[:, 0:C], "pp0", *side)
+            matmul(T.pp2[:, 0:b - a], "pp2", *side, not done, len(done) == NQ - 1)
+            done.append(i)
+
+        prev = None
+        for step in PLAN:
+            if step == "early":
+                if t == 0:
+                    add_base(FIRST, KB, [])
+                    settle(t, "pp0", FIRST, KB)
+            elif step == "tally":
+                do("v", ["zs:%d" % k for k in range(1, FROM_S)], ["cntv"], cp(T.cnt[:, 1:FROM_S], T.zs[:, 447:224 * FROM_S:224]))
+                add_base(0, FIRST if t == 0 else KB, ["cntv"])
+            elif step in ["q%d" % i for i in range(NQ)]:
+                sum_up(int(step[1]))
             else:
-                a, b, sgn, key, col = 0, 16 * k + 16, -1.0, "aw", T.aw
-            do("s", row + [key], ["rel%d" % i], act(T["rel%d" % i][:, a:b], T.srow[:, a:b], F.Relu, bias=col[:, k:k + 1], scale=sgn))
-            pend.append((k, i, a, b, sgn))
-            if n:
-                sign(*pend.pop(0))
-        sign(*pend.pop(0))
-        do("v", ["aw", "offl"] + row, ["eqr"], tt(T.eqr[:], T.aw[:, 0:KB].indirect(T.offl[:, 0:KB]), T.srow[:], A.is_equal))
-        shk = []
-        for i in range(HALF):
-            a, n, k = SLOT * i, 16 * (i + 1), KB - HALF + i
-            do("v", row + ["aw"], ["shb:%d" % i], ts(T.shb[:, a:a + n], T.srow[:, 0:n], T.aw[:, i:i + 1], A.is_ge))
-            shk.append("shb:%d" % i)
-            if k < KB - 1:
-                do("v", row + ["aw"], ["shb:h%d" % i], ts(T.shb[:, a + n:a + SLOT], T.srow[:, 16 * k + 16:C], T.aw[:, k:k + 1], A.is_gt))
-                shk.append("shb:h%d" % i)
-        do("v", ["eqr", "gateb"], ["eqs"], scan(T.eqs[:], T.gateb[:], T.eqr[:], 0.0, A.mult, A.add))
-        late = [
-            lambda: do("v", shk + ["sgate"], ["shs"], scan(T.shs[:], T.sgate[:], T.shb[:], 0.0, A.mult, A.add)),
-            lambda: do("v", ["eqs", "k0"], ["tc"], tt(T.tc[:], T.k0[:], T.eqs[:, 15:C:16], A.subtract)),
-            lambda: do("v", ["tc", "shs"], ["tc"], tt(T.tc[:, 0:HALF], T.tc[:, 0:HALF], T.shs[:, 15:SLOT * HALF:SLOT + 16], A.add)),
-            lambda: do("v", ["tc", "shs"], ["tc"], tt(T.tc[:, KB - HALF:KB - 1], T.tc[:, KB - HALF:KB - 1],
-                                                      T.shs[:, SLOT - 1:SLOT * (HALF - 1):SLOT], A.add)),
-        ]
-
-        def add_up(i):
-            bit = "bit%d" % (i % 4)
-            do("v", [bit + "l", bit + "r"], ["zs:%d" % i], scan(T.zs[:, 224 * i:224 * i + 224], T[bit][:, 0:224], T[bit][:, 224:C], -224.0, A.add, A.add))
-
-        for i in range(MID):
-            k = HALF + i
-            m, bit = 16 * k + 16, "bit%d" % (i % 4)
-            do("v", row + ["aw"], [bit + "l"], ts(T[bit][:, 0:m], T.srow[:, 0:m], T.aw[:, k:k + 1], A.is_ge))
-            do("v", row + ["aw"], [bit + "r"], ts(T[bit][:, m:C], T.srow[:, m:C], T.aw[:, k:k + 1], A.is_gt))
-            if i > 0:
-                add_up(i - 1)
-            if late:
-                late.pop(0)()
-            if t == 0 and i == EARLY:
-                settle(t, 0, HALF)
-        add_up(MID - 1)
-        do("v", ["zs:%d" % i for i in range(MID)], ["cntm"], cp(T.cnt[:, HALF:KB - HALF], T.zs[:, 223:224 * MID:224]))
-        settle(t, HALF if t == 0 else 0, KB)
+                k = step
+                do("v", row + ["aw"], ["fl%d" % k], ts(flags(k, 0, 16 * k + 16), T.srow[:, 0:16 * k + 16], T.aw[:, k:k + 1], A.is_ge))
+                if prev:
+                    add_up(prev)
+                prev = k
+                if k == FROM_S - 1:
+                    do("v", ["aw", "offl"] + row, ["eqr"], tt(T.eqr[:], T.aw[:, 0:KB].indirect(T.offl[:, 0:KB]), T.srow[:], A.is_equal))
+                if k == FROM_S - 2:
+                    do("v", ["eqr", "gatee"], ["eqs"], scan(T.eqs[:], T.gatee[:], T.eqr[:], 0.0, A.mult, A.add))
+                if k == FROM_S - 3:
+                    do("v", ["eqs"], ["tie"], ts(T.tie[:], T.eqs[:, 15:C:16], 1.0 / 64, A.mult, float(MAGIC), A.add))
+                    if t == 0:
+                        do("v", ["gs"], ["qg"], quant(T.qg[:], T.sg[:], T.gs[:]))
+                if k == FROM_S - 4:
+                    do("v", ["tie", "k0:0", "k0:v", "k0:s"], ["tie"], tt(T.tie[:], T.tie[:], T.k0[:], A.add))
+        settle(t, "pp2", 0, FIRST if t == 0 else KB)
 
     def wrap(row, key):
         do("v", [key, "ctl"], ["hrow"], scan(T.hrow[:], T.ctl[:], row, 0.0, A.add, A.max))
@@ -280,7 +303,7 @@ def rank_program(g, core, T, topo):
 
     def cycles(t):
         own, land = "own%d" % t, "land%d" % t
-        do("v", [own + ":0", own + ":%d" % HALF, "fh"], ["orow"], cp(T.orow[:, 0:C].indirect(T[own][:, 0:KB]), T.fh[:]))
+        do("v", [own + ":0", own + ":%d" % FIRST, "fh"], ["orow"], cp(T.orow[:, 0:C].indirect(T[own][:, 0:KB]), T.fh[:]))
         if t == 0:
             later_constants()
         do("s", ["orow", land], ["j0"], act(T.j0[:], T.orow[:, 0:C].indirect(T[land][:, 0:KB])))
@@ -302,7 +325,7 @@ def rank_program(g, core, T, topo):
                 do("v", ["hrow", "colj"], [o], ts(T[o][:], h, T.colj[:, 0:1], A.add))
         h = wrap(win[:], wkey)
         do("v", [wkey, "f15"], ["wrow"], scan(T.wrow[:], win[:], T.f15[:], -4.0, A.max, A.max))
-        do("v", ["hrow", "colm"], ["offm"], ts(T.offm[:], h, T.colm[:, 0:1], A.add, MAGIC, A.subtract))
+        do("v", ["hrow", "colm"], ["offm"], ts(T.offm[:], h, T.colm[:, 0:1], A.add, float(MAGIC), A.subtract))
         do("v", ["wrow", "f25"], ["crow"], scan(T.crow[:], T.wrow[:], T.f25[:], -2.5, A.add, A.subtract))
         do("v", ["crow", "offm", wkey], ["prow"], tt(T.prow[:], T.crow[:, 0:C].indirect(T.offm[:, 0:KB]), win[:], A.subtract))
         h = wrap(T.prow[:], "prow")
@@ -324,10 +347,12 @@ def rank_program(g, core, T, topo):
         zt, qz, sz = T["zt%d" % t], T["qz%d" % t], T["sz%d" % t]
         zk = ["z%d:%d:%d" % (t, h, i) for i in range(4)]
         do("v", zk, ["qz%d:%d" % (t, h)], quant(qz[:, a:b], sz[:, a:b], zt[:, 4 * a:4 * b]))
-        if h == 1:
-            do("v", zk, ["z64:%d" % h], ts(T.z64[:, 4 * a:4 * b], zt[:, 4 * a:4 * b], 64.0, A.mult))
-        else:
-            do("s", zk, ["z64:%d" % h], act(T.z64[:, 4 * a:4 * b], zt[:, 4 * a:4 * b], scale=64.0))
+        for i in range(4):
+            out, src, key = T.z64[:, 4 * a + i:4 * b:4], zt[:, 4 * a + i:4 * b:4], "z64:%d:%d" % (h, i)
+            if h == 1 and i % 2:
+                do("v", [zk[i]], [key], ts(out, src, 64.0, A.mult))
+            else:
+                do("s", [zk[i]], [key], act(out, src, scale=64.0))
         for i in range(4):
             matmul(T["pr%d" % i][:, 0:b - a], "pr%d" % i, T.qw[:, S * i:S * i + S], T.sw[:, S * i:S * i + S], ["w"],
                    qz[:, a:b], sz[:, a:b], ["qz%d:%d" % (t, h)])
@@ -335,25 +360,33 @@ def rank_program(g, core, T, topo):
     def sums(t, h, part):
         a, b = part
         for i in range(4):
-            do("v", ["pr%d" % i, "z64:%d" % h], ["r%d:%d" % (i, h)],
+            do("v", ["pr%d" % i, "z64:%d:%d" % (h, i)], ["r%d:%d" % (i, h)],
                tt(T["r%d" % i][:, a:b], T["pr%d" % i][:, 0:b - a], T.z64[:, 4 * a + i:4 * b:4], A.add))
-            do("s", ["r%d:%d" % (i, h)], ["x%d:%d:%d" % (t + 1, h, i)],
-               act(T["x%d" % (t + 1)][:, 4 * a + i:4 * b:4], T["r%d" % i][:, a:b], scale=0.015625))
+            out, src = T["x%d" % (t + 1)][:, 4 * a + i:4 * b:4], T["r%d" % i][:, a:b]
+            late = h == 2 and i == 3
+            do("v" if late else "s", ["r%d:%d" % (i, h)], ["x%d:%d:%d" % (t + 1, h, i)],
+               ts(out, src, 0.015625, A.mult) if late else act(out, src, scale=0.015625))
 
     def finish(t, h, part):
         a, b = part
         q, s, key, p = T["qx%d" % t], T["sx%d" % t], "qx%d:%d" % (t, h), "pp0" if h == 1 else "pp2"
         store("y", [key], T.oc[:, 4 * a:4 * b], q[:, a:b].bitcast(dt.uint8))
         matmul(T[p][:, 0:b - a], p, T.qv[:], T.sv[:], ["qv"], q[:, a:b], s[:, a:b], [key])
+
+    def store_rest(t, h, part):
+        a, b = part
+        s, key, p = T["sx%d" % t], "qx%d:%d" % (t, h), "pp0" if h == 1 else "pp2"
         do("s", [p], ["ysb:%d" % h], act(T.ysb[:, a:b], T[p][:, 0:b - a]))
+        store("s", ["ysb:%d" % h], T.y[:, a:b], T.ysb[:, a:b])
         for k in range(4):
             store("y", [key], T.osc[4 * k:4 * k + 4, a:b], s[32 * k:32 * k + 4, a:b])
-        store("s", ["ysb:%d" % h], T.y[:, a:b], T.ysb[:, a:b])
 
     quant_state(0, 1, H1)
     score(0, 1, H1)
     quant_state(0, 2, H2)
     score(0, 2, H2)
+    take_scores(0, 1, H1)
+    take_scores(0, 2, H2)
     for t in range(R):
         places(t)
         cycles(t)
@@ -373,9 +406,11 @@ def rank_program(g, core, T, topo):
         products(t, 2, H2)
         quant_state(t + 1, 1, H1)
         sums(t, 2, H2)
-        last = score if t < R - 1 else finish
+        last, then = (score, take_scores) if t < R - 1 else (finish, store_rest)
         last(t + 1, 1, H1)
         quant_state(t + 1, 2, H2)
         last(t + 1, 2, H2)
+        then(t + 1, 1, H1)
+        then(t + 1, 2, H2)
     for sem in sorted(count):
         g.wait_ge(T.sem[sem], count[sem])

@@ -6,13 +6,18 @@ KB = C // 16
 NQ = KB // 4
 WIDE = [max(128, 64 * (i + 1)) for i in range(NQ)]
 AT = [sum(WIDE[:i]) for i in range(NQ + 1)]
-FROM_S = 20
+BY_S = [27, 26, 25, 24, 23, 22, 21, 11, 10, 9, 8]
 FIRST = 24
-PLAN = [*range(19, 7, -1), "q6", 7, 6, 5, 4, "early", "q4", "q3", "q2", 3, 2, 1, 0, "q1", "tally", "q0", "q5"]
+HIGH = 12
+PLAN = [*range(20, 11, -1), "q6", 7, 6, 5, "q4", "early", "q3", 4, 3, 2, 1, 0, "q5", "q1", "q0", "tallyh", "high", "tallyl", "q2"]
+BY_V = sorted(k for k in PLAN if k in range(KB))
 ENGINES = 8
 H2, H1 = (0, S), (S, C)
+HALVES = {1: (S, S + 160), 3: (S + 160, C)}
+HALF = C // 2
+LIFT = 480
+OWN = 336
 MAGIC = 12582912
-LIFT, DROP = 512, 8192
 
 SCRATCH = {}
 
@@ -22,10 +27,12 @@ def _buf(dtype, n, *names):
         SCRATCH[name] = ("psum" if name[:2] in ("pp", "pr") and name[2:].isdigit() else "sbuf", [128, n], dtype)
 
 
-_buf("bfloat16", 512, "ub", "vb", "one", "go", "gs", "bt0", "bt1")
+_buf("bfloat16", 512, "ub", "vb", "one", "c64", "go", "gs", "bt0", "bt1")
 _buf("bfloat16", 4 * 512, "eb")
-_buf("bfloat16", C, "gatee", "eqr", "eqs", "rel0", "rel1", "rel2", "rel3")
-_buf("bfloat16", 224 * FROM_S, "zs")
+_buf("bfloat16", C, "mask", "gate", "gatee", "ctl", "ctlp", "fh", "orow", "prow", "erow", "j0", "j1",
+     "eqr", "eqs", "rel0", "rel1", "rel2", "rel3")
+_buf("float16", C, "hrow")
+_buf("bfloat16", 224 * KB, "zs")
 _buf("bfloat16", 4 * C, "z64", "x0", "x1", "x2", "zt0", "zt1")
 _buf("float8_e4m3fn_x4", 128, "qu", "qur", "qv", "qg", "qb0", "qb1", "qc0", "qc1")
 _buf("uint8", 128, "su", "sur", "sv", "sg", "sb0", "sb1", "sc0", "sc1")
@@ -39,13 +46,11 @@ _buf("uint8", AT[NQ], "sf")
 _buf("int32", C, "ci", "d15")
 _buf("int32", 8, "ku")
 _buf("int32", KB, "kl")
-_buf("int32", 2, "pc")
 _buf("uint16", 8, "offu")
 _buf("uint16", KB, "offl", "offm", "offp", "off0", "off1", "own0", "own1", "land0", "land1", "offe0", "offe1", "offe2", "offe3")
-_buf("float32", C, "mask", "gate", "ctl", "f0", "fh", "f15", "f25", "mrow", "arow", "srow", "orow", "hrow", "hcol",
-     "wrow", "crow", "prow", "erow", "ysb", "j0", "j1", "a0", "a1", "b0", "b1", "r0", "r1", "r2", "r3")
-_buf("float32", 8, "hold", "colj", "colm", "cole")
-_buf("float32", KB, "k0", "cnt", "tie", "base", "pl")
+_buf("float32", C, "thr", "thr1", "mrow", "arow", "srow", "hkey", "hcol", "wrow", "crow", "elf", "ysb",
+     "a0", "a1", "b0", "b1", "r0", "r1", "r2", "r3")
+_buf("float32", KB, "k0", "cnt", "tie", "base", "pl", "la", "lb", "lc")
 _buf("float32", 32, "aw")
 _buf("float32", 512, "pp0", "pp1", "pp2", "pp3", "pr0", "pr1", "pr2", "pr3")
 
@@ -153,56 +158,68 @@ def rank_program(g, core, T, topo):
     load("y", "ldw", 32, "w", T.sw[:], T.ws[:])
     load("y", "ldv", 16, "vb", T.vb[:], T.v[:])
 
+    iota("ci", [[-1, C]], C - 1, 1)
     iota("ku", [[16, 8]], 0, 0)
-    iota("ci", [[-1, C]], C, 1)
     iota("kl", [[1, KB]], 0, 0)
-    iota("pc", [[0, 2]], 0, 1)
-    iota("f0", [[1, C]], 0, 0)
-    low = C - 16 * (KB - FROM_S)
-    iota("k0", [[0, 1]], low - MAGIC, 0, slice(0, 1), "k0:0")
-    iota("k0", [[-16, FROM_S - 1]], low + 224 - 16 - MAGIC, 0, slice(1, FROM_S), "k0:v")
-    iota("k0", [[16, KB - FROM_S]], 16 * FROM_S - MAGIC, 0, slice(FROM_S, KB), "k0:s")
+    left, k0_keys = [], []
+    for k in range(KB):
+        n = C - 16 * k - 16 * sum(i >= k for i in BY_S) - LIFT - MAGIC
+        left.append(n + (16 * k if k in BY_S else HALF if k else 0))
+    k = 0
+    while k < KB:
+        step, n = (left[k + 1] - left[k] if 0 < k < KB - 1 else 0), 1
+        while 0 < k and k + n < KB and left[k + n] - left[k + n - 1] == step:
+            n += 1
+        k0_keys.append("k0:%d" % k)
+        iota("k0", [[step, n]], left[k], 0, slice(k, k + n), k0_keys[-1])
+        k += n
     do("v", [], ["one"], fill(T.one[:], 1.0))
-    do("v", ["ku"], ["offu"], cp(T.offu[:], T.ku[:]))
-    do("v", ["ci"], ["d15"], ts(T.d15[:], T.ci[:], 15, A.bitwise_and))
+    do("v", [], ["c64"], fill(T.c64[:], 64.0))
     do("v", [], ["cnt0"], fill(T.cnt[:, 0:1], 0.0))
-    do("v", ["d15"], ["mask"], ts(T.mask[:], T.d15[:], 0, A.is_equal))
-    do("v", ["d15"], ["gate"], ts(T.gate[:], T.d15[:], 0, A.not_equal))
+    do("v", ["ci"], ["d15"], ts(T.d15[:], T.ci[:], 15, A.bitwise_and))
+    do("v", ["d15"], ["ctl"], ts(T.ctl[:], T.d15[:], 64.0, A.mult, -float(LIFT), A.add))
+    do("v", ["ku"], ["offu"], cp(T.offu[:], T.ku[:]))
     do("v", ["ub"], ["qu"], quant(T.qu[:], T.su[:], T.ub[:]))
-    do("v", ["kl"], ["offl"], cp(T.offl[:], T.kl[:]))
+    do("v", ["ctl"], ["mask"], ts(T.mask[:], T.ctl[:], float(LIFT), A.is_equal))
     do("v", ["qu", "offu"], ["qur"], cp(T.qur[:, 0:128].bitcast(dt.uint32), T.qu[:, 0:128].bitcast(dt.uint32).indirect(T.offu[:, 0:8])))
     do("v", ["qu", "offu"], ["sur"], cp(T.sur[:, 0:128], T.su[:, 0:128].indirect(T.offu[:, 0:8])))
-    do("v", ["pc"], ["pc"], ts(T.pc[:], T.pc[:], 15, A.bitwise_and))
-    do("v", ["mask"], ["gatee"], ts(T.gatee[:], T.mask[:], 63.0, A.mult, 1.0, A.add))
-    do("v", ["mask"], ["ctl"], ts(T.ctl[:], T.mask[:], -float(LIFT + DROP), A.mult, float(LIFT), A.add))
-    do("v", ["gatee"], ["gatee"], fill(T.gatee[:, 0:C:16], 0.0))
-    do("v", ["pc"], ["hold"], ts(T.hold[:, 0:1], T.pc[:, 0:1], LIFT, A.mult, -15 * LIFT, A.add))
-    do("g", ["one"], ["go"], lambda e: e.affine_select(T.go[:], T.one[:], [[-16, 8], [0, 64]], A.is_ge, 0.0, 0, 1))
-    do("g", ["go"], ["gs"], lambda e: e.affine_select(T.gs[:], T.go[:], [[16, 8], [0, 64]], A.is_ge, 0.0, 15, -1))
-    for b in range(4):
-        do("g", ["one"], ["eb%d" % b], lambda e: e.affine_select(
-            T.eb[:, 512 * b:512 * b + 512], T.one[:], [[-1, 512]], A.is_equal, 0.0, b, 4))
+    do("v", ["ctl"], ["gate"], ts(T.gate[:], T.ctl[:], float(LIFT), A.not_equal))
+    do("v", ["kl"], ["offl"], cp(T.offl[:], T.kl[:]))
     for i in range(NQ):
         for j in range(64 * i, WIDE[i], 64):
             z = 4 * (AT[i] + j)
-            do("s", ["f0"], ["fl%d" % k for k in range(4 * i, 4 * i + 4)] if j == 64 * i else ["flz%d" % i],
-               act(T.fl[:, z:z + 256], T.f0[:, 0:256], scale=0.0))
-    for name, off in (("fh", -0.5), ("f15", -1.5), ("f25", -2.5)):
-        do("s", ["f0"], [name], act(T[name][:], T.f0[:], F.Identity, bias=off))
+            do("s", ["one"], ["fl%d" % k for k in range(4 * i, 4 * i + 4)] if j == 64 * i else ["flz%d" % i],
+               act(T.fl[:, z:z + 256], T.one[:, 0:256], scale=0.0))
+    do("s", ["mask"], ["gatee"], act(T.gatee[:], T.mask[:], F.Identity, scale=63.0, bias=1.0))
+    do("s", ["gatee"], ["gatee"], act(T.gatee[:, 0:C:16], T.one[:, 0:KB], scale=0.0))
+    do("g", ["one"], ["go"], lambda e: e.affine_select(T.go[:], T.one[:], [[-16, 8], [0, 64]], A.is_ge, 0.0, 0, 1))
+    do("g", ["go"], ["gs"], lambda e: e.affine_select(T.gs[:], T.go[:], [[16, 8], [0, 64]], A.is_ge, 0.0, 15, -1))
+    iota("fh", [[1, C]], -HALF, 0)
+    for b in range(4):
+        do("g", ["c64"], ["eb%d" % b], lambda e: e.affine_select(
+            T.eb[:, 512 * b:512 * b + 512], T.c64[:], [[-1, 512]], A.is_equal, 0.0, b, 4))
+
+    def block_ends():
+        q = T.d15[:, 15:C:16]
+        do("v", ["d15"], ["la"], ts(T.la[:], q, -1.0, A.mult, 15.0, A.add))
+        do("v", ["d15"], ["lb"], ts(T.lb[:], q, -32.0, A.mult, -32.0, A.add))
+        do("v", ["la", "lb"], ["lc"], tt(T.lc[:], T.la[:], T.lb[:], A.mult))
+        do("v", ["lc"], ["ctl"], ts(T.ctl[:, 15:C:16], T.lc[:], -float(LIFT), A.add))
 
     def later_constants():
-        do("v", ["hold"], ["colj"], ts(T.colj[:, 0:1], T.hold[:, 0:1], 0.5, A.add))
-        do("v", ["hold"], ["colm"], ts(T.colm[:, 0:1], T.hold[:, 0:1], float(MAGIC + 1), A.add))
-        for i in range(4):
-            do("v", ["hold"], ["cole%d" % i], ts(T.cole[:, i:i + 1], T.hold[:, 0:1], 0.25 * i, A.add))
         do("v", ["eb%d" % b for b in range(4)], ["qe"], quant(T.qe[:], T.se[:], T.eb[:]))
         do("v", ["vb"], ["qv"], quant(T.qv[:], T.sv[:], T.vb[:]))
+        do("s", ["fh"], ["thr"], act(T.thr[:], T.fh[:], F.Identity, bias=-0.5))
+        do("s", ["fh"], ["thr1"], act(T.thr1[:], T.fh[:], F.Identity, bias=-1.5))
+        do("s", ["ctl"], ["ctlp"], act(T.ctlp[:], T.ctl[:], scale=1.0 / 1024))
 
     def matmul(out, key, lhs, ls, lkey, rhs, rs, rkey, start=True, stop=True):
         do("t", lkey + rkey, [key], lambda e: e.matmul_mx(out, lhs, ls, rhs, rs, start, stop))
 
     def state_keys(t, h):
-        return ["x0:%d" % h] if t == 0 else ["x%d:%d:%d" % (t, h, i) for i in range(4)]
+        if t == 0:
+            return ["x0:%d" % h]
+        return ["x%d:%d:%d" % (t, h, i) for i in range(4)]
 
     def quant_state(t, h, part):
         a, b = part
@@ -221,15 +238,15 @@ def rank_program(g, core, T, topo):
         do("s", [p1], ["srow:%d" % h], act(T.srow[:, a:b], T[p1][:, 0:b - a]))
         do("v", ["mrow:%d" % h, "gate"], ["arow:%d" % h], scan(T.arow[:, a:b], T.gate[:, a:b], T.mrow[:, a:b], 0.0, A.mult, A.add))
 
-    def add_base(a, b, keys):
-        do("v", keys + ["cnt%d" % k for k in range(max(a, FROM_S), b)] + ["tie", "cnt0"], ["base:%d" % a],
-           tt(T.base[:, a:b], T.cnt[:, a:b], T.tie[:, a:b], A.add))
+    def add_base(a, b):
+        keys = ["cnt%d" % k if k in BY_S else "cntv%d" % (k >= HIGH) if k else "cnt0" for k in range(a, b)]
+        do("v", keys + ["tie"], ["base:%d" % a], tt(T.base[:, a:b], T.cnt[:, a:b], T.tie[:, a:b], A.add))
 
     def settle(t, bank, a, b):
-        do("v", [bank, "ctl"], ["hcol:%d" % a], scan(T.hcol[:, 16 * a:16 * b], T.ctl[:, 16 * a:16 * b], T[bank][:, 16 * a:16 * b], 0.0, A.add, A.max))
+        do("v", [bank, "ctl"], ["hcol:%d" % a], scan(T.hcol[:, 16 * a:16 * b], T[bank][:, 16 * a:16 * b], T.ctl[:, 16 * a:16 * b], -1024.0, A.max, A.add))
         do("v", ["hcol:%d" % a, "base:%d" % a], ["pl:%d" % a], tt(T.pl[:, a:b], T.base[:, a:b], T.hcol[:, 16 * a + 15:16 * b:16], A.subtract))
         key = "own%d:%d" % (t, a)
-        do("v", ["pl:%d" % a, "hold"], [key], ts(T["own%d" % t][:, a:b], T.pl[:, a:b], T.hold[:, 0:1], A.subtract))
+        do("v", ["pl:%d" % a], [key], cp(T["own%d" % t][:, a:b], T.pl[:, a:b]))
         send(t, [("land%d" % t, "own%d" % t, lambda n: T[n][:, a:b], key)], "rxi%d" % t)
 
     def places(t):
@@ -246,7 +263,7 @@ def rank_program(g, core, T, topo):
             do("s", [rel], ["fl%d" % k, "cnt%d" % k], act(flags(k, 0, 16 * k), T[rel][:, 0:16 * k], F.Sign, scale=-1.0, accum_out=T.cnt[:, k:k + 1]))
             do("s", [rel], ["fld%d" % k], act(flags(k, 16 * k, 16 * k + 16), T[rel][:, 16 * k:16 * k + 16], F.Sign, scale=-1.0))
 
-        for k in range(KB - 1, FROM_S - 1, -1):
+        for k in BY_S:
             rel = "rel%d" % (k % 4)
             do("s", row + ["aw"], [rel], act(T[rel][:, 0:16 * k + 16], T.srow[:, 0:16 * k + 16], F.Relu, bias=T.aw[:, k:k + 1], scale=-1.0))
             pend.append(k)
@@ -256,27 +273,51 @@ def rank_program(g, core, T, topo):
 
         def add_up(k):
             z = 224 * k + 224
-            do("v", ["fl%d" % k], ["zs:%d" % k], scan(T.zs[:, z - 8 * k:z], flags(k, 0, 8 * k), flags(k, 8 * k, 16 * k), -224.0, A.add, A.add))
+            do("v", ["fl%d" % k], ["zs:%d" % k], scan(T.zs[:, z - 8 * k:z], flags(k, 0, 8 * k), flags(k, 8 * k, 16 * k), -float(HALF), A.add, A.add))
+
+        def tally(a, b, n):
+            ks = [k for k in BY_V if a <= k < b]
+            at, runs = 0, []
+            while at < len(ks):
+                end = at
+                while end + 1 < len(ks) and ks[end + 1] == ks[end] + 1:
+                    end += 1
+                runs.append((ks[at], ks[end] + 1))
+                at = end + 1
+            for i, (c, d) in enumerate(runs):
+                key = "cntv%d" % n
+                do("v", ["zs:%d" % k for k in range(c, d)], [key] if i == len(runs) - 1 else [key + "'"],
+                   cp(T.cnt[:, c:d], T.zs[:, 224 * c + 223:224 * d:224]))
 
         def sum_up(i):
             a, b = AT[i], AT[i + 1]
             keys = [n % k for k in range(4 * i, 4 * i + 4) for n in ("fl%d", "fld%d")] + ["flz%d" % i]
             do("v", keys, ["qf%d" % i], quant(T.qf[:, a:b], T.sf[:, a:b], T.fl[:, 4 * a:4 * b]))
-            side = (T.qg[:], T.sg[:], ["qg"], T.qf[:, a:b], T.sf[:, a:b], ["qf%d" % i])
-            if t == 0 and i == NQ - 1:
-                matmul(T.pp0[:, 0:C], "pp0", *side)
-            matmul(T.pp2[:, 0:b - a], "pp2", *side, not done, len(done) == NQ - 1)
+
+            def add(bank, n, start, stop):
+                matmul(T[bank][:, 0:n], bank, T.qg[:], T.sg[:], ["qg"], T.qf[:, a:a + n], T.sf[:, a:a + n], ["qf%d" % i], start, stop)
+            last = len([j for j in done if j >= HIGH // 4]) == NQ - HIGH // 4 - 1
+            if i >= HIGH // 4:
+                if t == 0 and i == NQ - 1:
+                    add("pp0", C, True, True)
+                add("pp1", b - a, not done, last)
+            add("pp2", min(16 * HIGH, b - a), not done, len(done) == NQ - 1)
             done.append(i)
 
-        prev = None
+        prev, n = None, 0
         for step in PLAN:
             if step == "early":
                 if t == 0:
-                    add_base(FIRST, KB, [])
+                    add_base(FIRST, KB)
                     settle(t, "pp0", FIRST, KB)
-            elif step == "tally":
-                do("v", ["zs:%d" % k for k in range(1, FROM_S)], ["cntv"], cp(T.cnt[:, 1:FROM_S], T.zs[:, 447:224 * FROM_S:224]))
-                add_base(0, FIRST if t == 0 else KB, ["cntv"])
+            elif step == "tallyh":
+                tally(HIGH, KB, 1)
+                add_base(HIGH, FIRST if t == 0 else KB)
+            elif step == "high":
+                settle(t, "pp1", HIGH, FIRST if t == 0 else KB)
+            elif step == "tallyl":
+                tally(1, HIGH, 0)
+                add_base(0, HIGH)
             elif step in ["q%d" % i for i in range(NQ)]:
                 sum_up(int(step[1]))
             else:
@@ -285,55 +326,62 @@ def rank_program(g, core, T, topo):
                 if prev:
                     add_up(prev)
                 prev = k
-                if k == FROM_S - 1:
+                n += 1
+                if n == 1:
                     do("v", ["aw", "offl"] + row, ["eqr"], tt(T.eqr[:], T.aw[:, 0:KB].indirect(T.offl[:, 0:KB]), T.srow[:], A.is_equal))
-                if k == FROM_S - 2:
+                if n == 2:
                     do("v", ["eqr", "gatee"], ["eqs"], scan(T.eqs[:], T.gatee[:], T.eqr[:], 0.0, A.mult, A.add))
-                if k == FROM_S - 3:
+                if n == 3:
                     do("v", ["eqs"], ["tie"], ts(T.tie[:], T.eqs[:, 15:C:16], 1.0 / 64, A.mult, float(MAGIC), A.add))
                     if t == 0:
+                        block_ends()
                         do("v", ["gs"], ["qg"], quant(T.qg[:], T.sg[:], T.gs[:]))
-                if k == FROM_S - 4:
-                    do("v", ["tie", "k0:0", "k0:v", "k0:s"], ["tie"], tt(T.tie[:], T.tie[:], T.k0[:], A.add))
-        settle(t, "pp2", 0, FIRST if t == 0 else KB)
+                if n == 4:
+                    do("v", ["tie"] + k0_keys, ["tie"], tt(T.tie[:], T.tie[:], T.k0[:], A.add))
+        settle(t, "pp2", 0, HIGH)
 
-    def wrap(row, key):
-        do("v", [key, "ctl"], ["hrow"], scan(T.hrow[:], T.ctl[:], row, 0.0, A.add, A.max))
+    def wrap(row, key, ctl="ctl"):
+        do("v", [key, ctl], ["hrow"], scan(T.hrow[:], row, T[ctl][:], -1024.0, A.max, A.add))
         return T.hrow[:, 15:C:16]
+
+    def shifted(an, bn, d):
+        do("s", [an], [bn + ":s"], act(T[bn][:, 0:OWN], T[an][:, 0:OWN], F.Identity, bias=-d))
+        do("v", [an], [bn + ":v"], ts(T[bn][:, OWN:C], T[an][:, OWN:C], -d, A.add))
 
     def cycles(t):
         own, land = "own%d" % t, "land%d" % t
-        do("v", [own + ":0", own + ":%d" % FIRST, "fh"], ["orow"], cp(T.orow[:, 0:C].indirect(T[own][:, 0:KB]), T.fh[:]))
+        parts = [own + ":0", own + ":%d" % HIGH] + ([own + ":%d" % FIRST] if t == 0 else [])
+        do("v", parts + ["fh"], ["orow"], cp(T.orow[:, 0:C].indirect(T[own][:, 0:KB]), T.fh[:]))
         if t == 0:
             later_constants()
         do("s", ["orow", land], ["j0"], act(T.j0[:], T.orow[:, 0:C].indirect(T[land][:, 0:KB])))
-        do("s", ["j0"], ["b0"], act(T.b0[:], T.j0[:], F.Identity, bias=-1.0 / 512))
+        shifted("j0", "b0", 1.0 / 1024)
         h = wrap(T.j0[:], "j0")
-        do("v", ["hrow", "colj"], ["off0"], ts(T.off0[:], h, T.colj[:, 0:1], A.add))
+        do("v", ["hrow"], ["off0"], ts(T.off0[:], h, float(LIFT + HALF), A.add))
         win, wkey = T.j0, "j0"
         for k in range(9):
             off, j, jn = "off%d" % (k % 2), "j%d" % (k % 2), "j%d" % ((k + 1) % 2)
             an, bk, bn = "a%d" % (k % 2), "b%d" % (k % 2), "b%d" % ((k + 1) % 2)
             if k < 8:
                 do("s", [j, off], [jn], act(T[jn][:], T[j][:, 0:C].indirect(T[off][:, 0:KB])))
-            do("v", [wkey, off, bk], [an], tt(T[an][:], win[:, 0:C].indirect(T[off][:, 0:KB]), T[bk][:], A.min))
+            do("v", [wkey, off, bk + ":s", bk + ":v"], [an], tt(T[an][:], win[:, 0:C].indirect(T[off][:, 0:KB]), T[bk][:], A.min))
             win, wkey = T[an], an
             if k < 8:
-                do("s", [an], [bn], act(T[bn][:], T[an][:], F.Identity, bias=-(2.0 ** (k + 1)) / 512))
+                shifted(an, bn, (2.0 ** (k + 1)) / 1024)
                 h = wrap(T[jn][:], jn)
                 o = "off%d" % ((k + 1) % 2)
-                do("v", ["hrow", "colj"], [o], ts(T[o][:], h, T.colj[:, 0:1], A.add))
-        h = wrap(win[:], wkey)
-        do("v", [wkey, "f15"], ["wrow"], scan(T.wrow[:], win[:], T.f15[:], -4.0, A.max, A.max))
-        do("v", ["hrow", "colm"], ["offm"], ts(T.offm[:], h, T.colm[:, 0:1], A.add, float(MAGIC), A.subtract))
-        do("v", ["wrow", "f25"], ["crow"], scan(T.crow[:], T.wrow[:], T.f25[:], -2.5, A.add, A.subtract))
+                do("v", ["hrow"], [o], ts(T[o][:], h, float(LIFT + HALF), A.add))
+        do("v", [wkey, "ctl"], ["hkey"], scan(T.hkey[:], win[:], T.ctl[:], -1024.0, A.max, A.add))
+        do("v", [wkey, "thr"], ["wrow"], scan(T.wrow[:], win[:], T.thr[:], -1024.0, A.max, A.max))
+        do("v", ["hkey"], ["offm"], ts(T.offm[:], T.hkey[:, 15:C:16], float(MAGIC + LIFT + HALF), A.add, float(MAGIC), A.subtract))
+        do("v", ["wrow", "thr1"], ["crow"], scan(T.crow[:], T.wrow[:], T.thr1[:], -HALF - 1.5 - HALF / 1024, A.add, A.subtract))
         do("v", ["crow", "offm", wkey], ["prow"], tt(T.prow[:], T.crow[:, 0:C].indirect(T.offm[:, 0:KB]), win[:], A.subtract))
-        h = wrap(T.prow[:], "prow")
-        do("v", ["hrow", "hold"], ["offp"], ts(T.offp[:], h, T.hold[:, 0:1], A.add, 512.0, A.mult))
-        do("v", ["offp", "f0"], ["erow"], cp(T.erow[:, 0:C].indirect(T.offp[:, 0:KB]), T.f0[:]))
+        h = wrap(T.prow[:], "prow", "ctlp")
+        do("v", ["hrow"], ["offp"], ts(T.offp[:], h, (LIFT + HALF) / 1024, A.add, 1024.0, A.mult))
+        do("v", ["offp", "fh"], ["erow"], cp(T.erow[:, 0:C].indirect(T.offp[:, 0:KB]), T.fh[:]))
         h = wrap(T.erow[:], "erow")
         for i in (2, 0, 3, 1):
-            do("v", ["hrow", "cole%d" % i], ["offe%d" % i], ts(T["offe%d" % i][:], h, T.cole[:, i:i + 1], A.add, 4.0, A.mult))
+            do("v", ["hrow"], ["offe%d" % i], ts(T["offe%d" % i][:], h, LIFT + HALF + 0.25 * i, A.add, 4.0, A.mult))
 
     def lay_out(t, tile, key, part):
         a, b = part
@@ -342,30 +390,51 @@ def rank_program(g, core, T, topo):
             src = T["x%d" % t][:, 0:4 * C].indirect(T["offe%d" % i][:, a // 16:b // 16])
             do("v" if i < 2 else "s", state_keys(t, 1) + state_keys(t, 2) + ["offe%d" % i], [key + str(i)], cp(out, src) if i < 2 else act(out, src))
 
-    def products(t, h, part):
-        a, b = part
-        zt, qz, sz = T["zt%d" % t], T["qz%d" % t], T["sz%d" % t]
-        zk = ["z%d:%d:%d" % (t, h, i) for i in range(4)]
-        do("v", zk, ["qz%d:%d" % (t, h)], quant(qz[:, a:b], sz[:, a:b], zt[:, 4 * a:4 * b]))
-        for i in range(4):
-            out, src, key = T.z64[:, 4 * a + i:4 * b:4], zt[:, 4 * a + i:4 * b:4], "z64:%d:%d" % (h, i)
-            if h == 1 and i % 2:
-                do("v", [zk[i]], [key], ts(out, src, 64.0, A.mult))
-            else:
-                do("s", [zk[i]], [key], act(out, src, scale=64.0))
-        for i in range(4):
-            matmul(T["pr%d" % i][:, 0:b - a], "pr%d" % i, T.qw[:, S * i:S * i + S], T.sw[:, S * i:S * i + S], ["w"],
-                   qz[:, a:b], sz[:, a:b], ["qz%d:%d" % (t, h)])
+    def layer(t, i, qz, sz, a, b, key, bank, start=True):
+        matmul(T[bank][:, 0:b - a], bank, T.qw[:, S * i:S * i + S], T.sw[:, S * i:S * i + S], ["w"], qz[:, a:b], sz[:, a:b], [key], start, True)
 
-    def sums(t, h, part):
-        a, b = part
+    def stay(t):
+        zt, qz, sz, xn = T["zt%d" % t], T["qz%d" % t], T["sz%d" % t], T["x%d" % (t + 1)]
+        for h, (a, b) in HALVES.items():
+            zk = "z%d:%d:" % (t, h)
+            lay_out(t, zt, zk, (a, b))
+            do("v", [zk + str(i) for i in range(4)], ["qz%d:%d" % (t, h)], quant(qz[:, a:b], sz[:, a:b], zt[:, 4 * a:4 * b]))
+            for i in range(4):
+                layer(t, i, qz, sz, a, b, "qz%d:%d" % (t, h), ("pr%d" if h == 1 else "pp%d") % i)
+        a, b = H1
         for i in range(4):
-            do("v", ["pr%d" % i, "z64:%d:%d" % (h, i)], ["r%d:%d" % (i, h)],
-               tt(T["r%d" % i][:, a:b], T["pr%d" % i][:, 0:b - a], T.z64[:, 4 * a + i:4 * b:4], A.add))
-            out, src = T["x%d" % (t + 1)][:, 4 * a + i:4 * b:4], T["r%d" % i][:, a:b]
-            late = h == 2 and i == 3
-            do("v" if late else "s", ["r%d:%d" % (i, h)], ["x%d:%d:%d" % (t + 1, h, i)],
-               ts(out, src, 0.015625, A.mult) if late else act(out, src, scale=0.015625))
+            out, src = T.z64[:, 4 * a + i:4 * b:4], zt[:, 4 * a + i:4 * b:4]
+            reads = ["z%d:%d:%d" % (t, h, i) for h in HALVES]
+            do("v" if i % 2 else "s", reads, ["z64:%d" % i], ts(out, src, 64.0, A.mult) if i % 2 else act(out, src, scale=64.0))
+        for h, (a, b) in HALVES.items():
+            for i in range(4):
+                bank = ("pr%d" if h == 1 else "pp%d") % i
+                do("v", [bank, "z64:%d" % i], ["r%d:%d" % (i, h)],
+                   tt(T["r%d" % i][:, a:b], T[bank][:, 0:b - a], T.z64[:, 4 * a + i:4 * b:4], A.add))
+        a, b = H1
+        for i in range(4):
+            do("s", ["r%d:%d" % (i, h) for h in HALVES], ["x%d:1:%d" % (t + 1, i)], act(xn[:, 4 * a + i:4 * b:4], T["r%d" % i][:, a:b], scale=0.015625))
+
+    def unpack(t, i, start, stop):
+        qc, sc = "qc%d" % t, "sc%d" % t
+        matmul(T["pr%d" % i][:, 0:S], "pr%d" % i, T.qe[:, S * i:S * i + S], T.se[:, S * i:S * i + S], ["qe"], T[qc][:], T[sc][:], [qc, sc], start, stop)
+
+    def arrive(t):
+        zt, qz, sz = T["zt%d" % t], T["qz%d" % t], T["sz%d" % t]
+        for i in range(4):
+            unpack(t, i, True, True)
+            do("v", ["pr%d" % i], ["z%d:2:%d" % (t, i)], ts(zt[:, i:4 * S:4], T["pr%d" % i][:, 0:S], 0.015625, A.mult))
+        do("v", ["z%d:2:%d" % (t, i) for i in range(4)], ["qz%d:2" % t], quant(qz[:, 0:S], sz[:, 0:S], zt[:, 0:4 * S]))
+        for i in range(4):
+            unpack(t, i, True, False)
+        for i in range(4):
+            layer(t, i, qz, sz, 0, S, "qz%d:2" % t, "pr%d" % i, False)
+
+    def arrived(t):
+        for i in range(4):
+            out, src = T["x%d" % (t + 1)][:, i:4 * S:4], T["pr%d" % i][:, 0:S]
+            do("s" if i < 2 else "v", ["pr%d" % i], ["x%d:2:%d" % (t + 1, i)],
+               act(out, src, scale=0.015625) if i < 2 else ts(out, src, 0.015625, A.mult))
 
     def finish(t, h, part):
         a, b = part
@@ -390,22 +459,17 @@ def rank_program(g, core, T, topo):
     for t in range(R):
         places(t)
         cycles(t)
-        if t == R - 1:
-            store("y", ["erow"], T.el[:], T.erow[0:128:16, :])
         bt, qb, sb, qc, sc = ["%s%d" % (n, t) for n in ("bt", "qb", "sb", "qc", "sc")]
         lay_out(t, T[bt], bt + ":", H2)
         do("v", [bt + ":%d" % i for i in range(4)], [qb, sb], quant(T[qb][:], T[sb][:], T[bt][:]))
         send(t, [(qc, qb, lambda n: T[n][:].bitcast(dt.uint8), qb), (sc, sb, lambda n: T[n][:], sb)], "rxb%d" % t)
-        lay_out(t, T["zt%d" % t], "z%d:1:" % t, H1)
-        products(t, 1, H1)
-        sums(t, 1, H1)
-        for i in (2, 0, 3, 1):
-            matmul(T["pr%d" % i][:, 0:S], "pr%d" % i, T.qe[:, S * i:S * i + S], T.se[:, S * i:S * i + S], ["qe"], T[qc][:], T[sc][:], [qc, sc])
-            out, src = T["zt%d" % t][:, i:4 * S:4], T["pr%d" % i][:, 0:S]
-            do("v" if i < 2 else "s", ["pr%d" % i], ["z%d:2:%d" % (t, i)], cp(out, src) if i < 2 else act(out, src))
-        products(t, 2, H2)
+        stay(t)
+        if t == R - 1:
+            do("s", ["erow"], ["elf"], act(T.elf[:], T.erow[:], F.Identity, bias=float(HALF)))
+            store("y", ["elf"], T.el[:], T.elf[0:128:16, :])
+        arrive(t)
         quant_state(t + 1, 1, H1)
-        sums(t, 2, H2)
+        arrived(t)
         last, then = (score, take_scores) if t < R - 1 else (finish, store_rest)
         last(t + 1, 1, H1)
         quant_state(t + 1, 2, H2)

@@ -6,17 +6,21 @@ KB = C // 16
 NQ = KB // 4
 WIDE = [max(128, 64 * (i + 1)) for i in range(NQ)]
 AT = [sum(WIDE[:i]) for i in range(NQ + 1)]
-BY_S = [27, 26, 25, 24, 23, 22, 21, 11, 10, 9, 8]
+BY_S = [27, 26, 25, 24, 7, 22, 21, 11, 10, 9, 8]
 FIRST = 24
 HIGH = 12
-PLAN = [*range(20, 11, -1), "q6", 7, 6, 5, "q4", "early", "q3", 4, 3, 2, 1, 0, "q5", "q1", "q0", "tallyh", "high", "tallyl", "q2"]
+PLAN = [*range(20, 12, -1), 6, 12, "q6", "q3", 23, 5, "q4", "early", 4, 3, 2, "q5", 1, 0, "q1", "tallyh", "c", "q2", "high", "q0",
+        "tallyl", "c"]
 BY_V = sorted(k for k in PLAN if k in range(KB))
 ENGINES = 8
 H2, H1 = (0, S), (S, C)
 HALVES = {1: (S, S + 160), 3: (S + 160, C)}
 HALF = C // 2
 LIFT = 480
-OWN = 336
+DEEP = 1024
+CUT = (320, 384)
+LOW = 96
+ENDS = 224
 MAGIC = 12582912
 
 SCRATCH = {}
@@ -27,9 +31,9 @@ def _buf(dtype, n, *names):
         SCRATCH[name] = ("psum" if name[:2] in ("pp", "pr") and name[2:].isdigit() else "sbuf", [128, n], dtype)
 
 
-_buf("bfloat16", 512, "ub", "vb", "one", "c64", "go", "gs", "bt0", "bt1")
+_buf("bfloat16", 512, "ub", "vb", "neg", "c64", "go", "gs", "bt0", "bt1")
 _buf("bfloat16", 4 * 512, "eb")
-_buf("bfloat16", C, "mask", "gate", "gatee", "ctl", "ctlp", "fh", "orow", "prow", "erow", "j0", "j1",
+_buf("bfloat16", C, "mask", "gate", "ctl", "ctlp", "fh", "orow", "crow", "prow", "erow", "j0", "j1",
      "eqr", "eqs", "rel0", "rel1", "rel2", "rel3")
 _buf("float16", C, "hrow")
 _buf("bfloat16", 224 * KB, "zs")
@@ -45,17 +49,16 @@ _buf("float8_e4m3fn_x4", AT[NQ], "qf")
 _buf("uint8", AT[NQ], "sf")
 _buf("int32", C, "ci", "d15")
 _buf("int32", 8, "ku")
-_buf("int32", KB, "kl")
 _buf("uint16", 8, "offu")
-_buf("uint16", KB, "offl", "offm", "offp", "off0", "off1", "own0", "own1", "land0", "land1", "offe0", "offe1", "offe2", "offe3")
-_buf("float32", C, "thr", "thr1", "mrow", "arow", "srow", "hkey", "hcol", "wrow", "crow", "elf", "ysb",
+_buf("uint16", KB, "offm", "offp", "off0", "off1", "own0", "own1", "land0", "land1", "offe0", "offe1", "offe2", "offe3")
+_buf("float32", C, "thr", "mrow", "arow", "srow", "ctlb", "hkey", "hcol", "wrow", "elf", "ysb",
      "a0", "a1", "b0", "b1", "r0", "r1", "r2", "r3")
-_buf("float32", KB, "k0", "cnt", "tie", "base", "pl", "la", "lb", "lc")
+_buf("float32", KB, "k0", "k1", "cnt", "tie", "la", "lb", "lc", "mw", "kw", "pw")
 _buf("float32", 32, "aw")
 _buf("float32", 512, "pp0", "pp1", "pp2", "pp3", "pr0", "pr1", "pr2", "pr3")
 
 LOADS = ["ldu", "ldx1", "ldx2", "ldw", "ldv"]
-SEMAPHORES = ["cv", "cs", "ct", "cg", "stored", "sent", "rxi0", "rxi1", "rxb0", "rxb1"] + LOADS
+SEMAPHORES = ["cv", "cs", "ct", "cg", "stored", "sent", "rxh0", "rxh1", "rxl0", "rxl1", "rxb0", "rxb1"] + LOADS
 
 
 def rank_program(g, core, T, topo):
@@ -116,11 +119,11 @@ def rank_program(g, core, T, topo):
         eng = topo.engines(core, dst)[:ENGINES]
         mask = sum(1 << e for e in eng)
         total = count.get(sem, 0) + len(pairs) * len(eng)
-        for there, here, view, key in pairs:
+        for land, there, here, view, key in pairs:
             before("g", [key], [])
             g.remote_dma(view(there), view(here), T.sem[sem], T.sem["sent"], pid, rid, mask)
             count["sent"] = count.get("sent", 0) + len(eng)
-            writer[there] = [("far", sem, total, {})]
+            writer[land] = [("far", sem, total, {})]
         count[sem] = total
 
     def ts(out, in0, s1, op0, s2=None, op1=None):
@@ -146,6 +149,9 @@ def rank_program(g, core, T, topo):
     def scan(out, d0, d1, init, op0, op1):
         return lambda e: e.tensor_tensor_scan(out, d0, d1, init, op0, op1)
 
+    def back(a, b):
+        return slice(b - 1, a - 1 if a else None, -1)
+
     def iota(name, pattern, base, cm, cols=slice(None), key=None):
         kw = {} if SCRATCH[name][2] == "int32" else {"allow_small_or_imprecise_dtypes": True}
         do("g", [], [key or name], lambda e: e.iota(T[name][:, cols], pattern, base, cm, **kw))
@@ -160,10 +166,12 @@ def rank_program(g, core, T, topo):
 
     iota("ci", [[-1, C]], C - 1, 1)
     iota("ku", [[16, 8]], 0, 0)
-    iota("kl", [[1, KB]], 0, 0)
+    do("v", [], ["neg"], fill(T.neg[:], -1.0))
+    do("g", ["neg"], ["go"], lambda e: e.affine_select(T.go[:], T.neg[:], [[-16, 8], [0, 64]], A.is_ge, 0.0, 0, 1))
+    do("g", ["go"], ["gs"], lambda e: e.affine_select(T.gs[:], T.go[:], [[16, 8], [0, 64]], A.is_ge, 0.0, 15, -1))
     left, k0_keys = [], []
     for k in range(KB):
-        n = C - 16 * k - 16 * sum(i >= k for i in BY_S) - LIFT - MAGIC
+        n = C - 16 * k - 16 * sum(i >= k for i in BY_S) - 1 - DEEP
         left.append(n + (16 * k if k in BY_S else HALF if k else 0))
     k = 0
     while k < KB:
@@ -173,45 +181,36 @@ def rank_program(g, core, T, topo):
         k0_keys.append("k0:%d" % k)
         iota("k0", [[step, n]], left[k], 0, slice(k, k + n), k0_keys[-1])
         k += n
-    do("v", [], ["one"], fill(T.one[:], 1.0))
     do("v", [], ["c64"], fill(T.c64[:], 64.0))
     do("v", [], ["cnt0"], fill(T.cnt[:, 0:1], 0.0))
     do("v", ["ci"], ["d15"], ts(T.d15[:], T.ci[:], 15, A.bitwise_and))
     do("v", ["d15"], ["ctl"], ts(T.ctl[:], T.d15[:], 64.0, A.mult, -float(LIFT), A.add))
+    own_q = T.d15[:, 15:C:16]
+    do("v", ["d15"], ["la"], ts(T.la[:], own_q, -1.0, A.mult, 15.0, A.add))
+    do("v", ["d15"], ["lb"], ts(T.lb[:], own_q, -32.0, A.mult, -32.0, A.add))
+    do("v", ["ctl"], ["mask"], ts(T.mask[:], T.ctl[:], float(LIFT), A.is_equal))
+    do("v", ["la", "lb"], ["lc"], tt(T.lc[:], T.la[:], T.lb[:], A.mult))
+    do("v", ["ctl"], ["gate"], ts(T.gate[:], T.ctl[:], float(LIFT), A.not_equal))
+    do("v", ["lc"], ["ctl"], ts(T.ctl[:, 15:C:16], T.lc[:], -float(LIFT), A.add))
     do("v", ["ku"], ["offu"], cp(T.offu[:], T.ku[:]))
     do("v", ["ub"], ["qu"], quant(T.qu[:], T.su[:], T.ub[:]))
-    do("v", ["ctl"], ["mask"], ts(T.mask[:], T.ctl[:], float(LIFT), A.is_equal))
     do("v", ["qu", "offu"], ["qur"], cp(T.qur[:, 0:128].bitcast(dt.uint32), T.qu[:, 0:128].bitcast(dt.uint32).indirect(T.offu[:, 0:8])))
     do("v", ["qu", "offu"], ["sur"], cp(T.sur[:, 0:128], T.su[:, 0:128].indirect(T.offu[:, 0:8])))
-    do("v", ["ctl"], ["gate"], ts(T.gate[:], T.ctl[:], float(LIFT), A.not_equal))
-    do("v", ["kl"], ["offl"], cp(T.offl[:], T.kl[:]))
     for i in range(NQ):
         for j in range(64 * i, WIDE[i], 64):
             z = 4 * (AT[i] + j)
-            do("s", ["one"], ["fl%d" % k for k in range(4 * i, 4 * i + 4)] if j == 64 * i else ["flz%d" % i],
-               act(T.fl[:, z:z + 256], T.one[:, 0:256], scale=0.0))
-    do("s", ["mask"], ["gatee"], act(T.gatee[:], T.mask[:], F.Identity, scale=63.0, bias=1.0))
-    do("s", ["gatee"], ["gatee"], act(T.gatee[:, 0:C:16], T.one[:, 0:KB], scale=0.0))
-    do("g", ["one"], ["go"], lambda e: e.affine_select(T.go[:], T.one[:], [[-16, 8], [0, 64]], A.is_ge, 0.0, 0, 1))
-    do("g", ["go"], ["gs"], lambda e: e.affine_select(T.gs[:], T.go[:], [[16, 8], [0, 64]], A.is_ge, 0.0, 15, -1))
+            do("s", ["neg"], ["fl%d" % k for k in range(4 * i, 4 * i + 4)] if j == 64 * i else ["flz%d" % i],
+               act(T.fl[:, z:z + 256], T.neg[:, 0:256], scale=0.0))
+    do("s", ["ctl"], ["ctlb"], act(T.ctlb[:], T.ctl[:]))
     iota("fh", [[1, C]], -HALF, 0)
     for b in range(4):
         do("g", ["c64"], ["eb%d" % b], lambda e: e.affine_select(
             T.eb[:, 512 * b:512 * b + 512], T.c64[:], [[-1, 512]], A.is_equal, 0.0, b, 4))
 
-    def block_ends():
-        q = T.d15[:, 15:C:16]
-        do("v", ["d15"], ["la"], ts(T.la[:], q, -1.0, A.mult, 15.0, A.add))
-        do("v", ["d15"], ["lb"], ts(T.lb[:], q, -32.0, A.mult, -32.0, A.add))
-        do("v", ["la", "lb"], ["lc"], tt(T.lc[:], T.la[:], T.lb[:], A.mult))
-        do("v", ["lc"], ["ctl"], ts(T.ctl[:, 15:C:16], T.lc[:], -float(LIFT), A.add))
+    def quant_const(b):
+        do("v", ["eb%d" % b], ["qe%d" % b], quant(T.qe[:, S * b:S * b + S], T.se[:, S * b:S * b + S], T.eb[:, 512 * b:512 * b + 512]))
 
-    def later_constants():
-        do("v", ["eb%d" % b for b in range(4)], ["qe"], quant(T.qe[:], T.se[:], T.eb[:]))
-        do("v", ["vb"], ["qv"], quant(T.qv[:], T.sv[:], T.vb[:]))
-        do("s", ["fh"], ["thr"], act(T.thr[:], T.fh[:], F.Identity, bias=-0.5))
-        do("s", ["fh"], ["thr1"], act(T.thr1[:], T.fh[:], F.Identity, bias=-1.5))
-        do("s", ["ctl"], ["ctlp"], act(T.ctlp[:], T.ctl[:], scale=1.0 / 1024))
+    later = [lambda b=b: quant_const(b) for b in range(4)] + [lambda: do("v", ["vb"], ["qv"], quant(T.qv[:], T.sv[:], T.vb[:]))]
 
     def matmul(out, key, lhs, ls, lkey, rhs, rs, rkey, start=True, stop=True):
         do("t", lkey + rkey, [key], lambda e: e.matmul_mx(out, lhs, ls, rhs, rs, start, stop))
@@ -219,7 +218,7 @@ def rank_program(g, core, T, topo):
     def state_keys(t, h):
         if t == 0:
             return ["x0:%d" % h]
-        return ["x%d:%d:%d" % (t, h, i) for i in range(4)]
+        return ["x%d:%d:%d" % (t, c, i) for c in ((1, 3) if h == 1 else (2,)) for i in range(4)]
 
     def quant_state(t, h, part):
         a, b = part
@@ -236,22 +235,22 @@ def rank_program(g, core, T, topo):
         p0, p1 = ("pp0", "pp1") if h == 1 else ("pp2", "pp3")
         do("v", [p0, "mask"], ["mrow:%d" % h], tt(T.mrow[:, a:b], T[p0][:, 0:b - a], T.mask[:, a:b], A.mult))
         do("s", [p1], ["srow:%d" % h], act(T.srow[:, a:b], T[p1][:, 0:b - a]))
-        do("v", ["mrow:%d" % h, "gate"], ["arow:%d" % h], scan(T.arow[:, a:b], T.gate[:, a:b], T.mrow[:, a:b], 0.0, A.mult, A.add))
+        do("v", ["mrow:%d" % h, "gate"], ["arow:%d" % h], scan(T.arow[:, back(a, b)], T.gate[:, back(a, b)], T.mrow[:, back(a, b)], 0.0, A.mult, A.add))
 
     def add_base(a, b):
         keys = ["cnt%d" % k if k in BY_S else "cntv%d" % (k >= HIGH) if k else "cnt0" for k in range(a, b)]
-        do("v", keys + ["tie"], ["base:%d" % a], tt(T.base[:, a:b], T.cnt[:, a:b], T.tie[:, a:b], A.add))
+        do("v", keys + ["tie", "ctlb"], ["ctlb:%d" % a], tt(T.ctlb[:, 16 * a + 15:16 * b:16], T.cnt[:, a:b], T.tie[:, a:b], A.add))
 
     def settle(t, bank, a, b):
-        do("v", [bank, "ctl"], ["hcol:%d" % a], scan(T.hcol[:, 16 * a:16 * b], T[bank][:, 16 * a:16 * b], T.ctl[:, 16 * a:16 * b], -1024.0, A.max, A.add))
-        do("v", ["hcol:%d" % a, "base:%d" % a], ["pl:%d" % a], tt(T.pl[:, a:b], T.base[:, a:b], T.hcol[:, 16 * a + 15:16 * b:16], A.subtract))
+        do("v", [bank, "ctlb:%d" % a], ["hcol:%d" % a], scan(T.hcol[:, 16 * a:16 * b], T[bank][:, 16 * a:16 * b], T.ctlb[:, 16 * a:16 * b], -float(DEEP), A.max, A.add))
         key = "own%d:%d" % (t, a)
-        do("v", ["pl:%d" % a], [key], cp(T["own%d" % t][:, a:b], T.pl[:, a:b]))
-        send(t, [("land%d" % t, "own%d" % t, lambda n: T[n][:, a:b], key)], "rxi%d" % t)
+        do("v", ["hcol:%d" % a], [key], ts(T["own%d" % t][:, a:b], T.hcol[:, 16 * a + 15:16 * b:16], float(DEEP), A.add))
+        h = "h" if a >= HIGH else "l"
+        send(t, [("land%d:%s" % (t, h), "land%d" % t, "own%d" % t, lambda n: T[n][:, a:b], key)], "rx%s%d" % (h, t))
 
     def places(t):
         row = ["srow:1", "srow:2"]
-        do("v", ["arow:1", "arow:2"], ["aw"], cp(T.aw[:, 0:KB], T.arow[:, 15:C:16]))
+        do("v", ["arow:1", "arow:2"], ["aw"], cp(T.aw[:, 0:KB], T.arow[:, 0:C:16]))
         pend, done = [], []
 
         def flags(k, a, b):
@@ -299,17 +298,20 @@ def rank_program(g, core, T, topo):
             last = len([j for j in done if j >= HIGH // 4]) == NQ - HIGH // 4 - 1
             if i >= HIGH // 4:
                 if t == 0 and i == NQ - 1:
-                    add("pp0", C, True, True)
-                add("pp1", b - a, not done, last)
+                    add("pp3", C, True, True)
+                add("pp1", b - a, not any(j >= HIGH // 4 for j in done), last)
             add("pp2", min(16 * HIGH, b - a), not done, len(done) == NQ - 1)
             done.append(i)
 
         prev, n = None, 0
         for step in PLAN:
-            if step == "early":
+            if step == "c":
+                for _ in range(2 if t == 0 else 0):
+                    later.pop(0)()
+            elif step == "early":
                 if t == 0:
                     add_base(FIRST, KB)
-                    settle(t, "pp0", FIRST, KB)
+                    settle(t, "pp3", FIRST, KB)
             elif step == "tallyh":
                 tally(HIGH, KB, 1)
                 add_base(HIGH, FIRST if t == 0 else KB)
@@ -328,60 +330,91 @@ def rank_program(g, core, T, topo):
                 prev = k
                 n += 1
                 if n == 1:
-                    do("v", ["aw", "offl"] + row, ["eqr"], tt(T.eqr[:], T.aw[:, 0:KB].indirect(T.offl[:, 0:KB]), T.srow[:], A.is_equal))
+                    for h, p, (a, b) in ((1, "pp0", H1), (2, "pp2", H2)):
+                        do("v", ["arow:%d" % h, p], ["eqr:%d" % h], tt(T.eqr[:, a:b], T.arow[:, a:b], T[p][:, 0:b - a], A.is_equal))
                 if n == 2:
-                    do("v", ["eqr", "gatee"], ["eqs"], scan(T.eqs[:], T.gatee[:], T.eqr[:], 0.0, A.mult, A.add))
-                if n == 3:
-                    do("v", ["eqs"], ["tie"], ts(T.tie[:], T.eqs[:, 15:C:16], 1.0 / 64, A.mult, float(MAGIC), A.add))
+                    do("v", ["eqr:1", "eqr:2", "gate"], ["eqs"], scan(T.eqs[:, back(0, C)], T.gate[:, back(0, C)], T.eqr[:, back(0, C)], 0.0, A.mult, A.add))
                     if t == 0:
-                        block_ends()
-                        do("v", ["gs"], ["qg"], quant(T.qg[:], T.sg[:], T.gs[:]))
-                if n == 4:
-                    do("v", ["tie"] + k0_keys, ["tie"], tt(T.tie[:], T.tie[:], T.k0[:], A.add))
+                        do("v", ["lc"] + k0_keys, ["k1"], tt(T.k1[:], T.lc[:], T.k0[:], A.add))
+                if n == 3:
+                    do("v", ["eqs", "k1"], ["tie"], tt(T.tie[:], T.eqs[:, 0:C:16], T.k1[:], A.add))
         settle(t, "pp2", 0, HIGH)
 
-    def wrap(row, key, ctl="ctl"):
-        do("v", [key, ctl], ["hrow"], scan(T.hrow[:], row, T[ctl][:], -1024.0, A.max, A.add))
-        return T.hrow[:, 15:C:16]
+    def wrap(row, keys, part=(0, C), ctl="ctl", to=("hrow:l", "hrow:h")):
+        a, b = part
+        do("v", keys + [ctl], list(to), scan(T.hrow[:, a:b], row[:, a:b], T[ctl][:, a:b], -1024.0, A.max, A.add))
+        return T.hrow[:, a + 15:b:16]
 
-    def shifted(an, bn, d):
-        do("s", [an], [bn + ":s"], act(T[bn][:, 0:OWN], T[an][:, 0:OWN], F.Identity, bias=-d))
-        do("v", [an], [bn + ":v"], ts(T[bn][:, OWN:C], T[an][:, OWN:C], -d, A.add))
+    def three(name):
+        return [name + ":s", name + ":v", name + ":h"]
+
+    def both(name):
+        return [name + ":l", name + ":h"]
+
+    def shift(q, an, keys, bn, d, a, b):
+        do(q, keys, [bn + ":%d" % a], act(T[bn][:, a:b], T[an][:, a:b], F.Identity, bias=-d) if q == "s"
+           else ts(T[bn][:, a:b], T[an][:, a:b], -d, A.add))
+        return bn + ":%d" % a
 
     def cycles(t):
         own, land = "own%d" % t, "land%d" % t
         parts = [own + ":0", own + ":%d" % HIGH] + ([own + ":%d" % FIRST] if t == 0 else [])
         do("v", parts + ["fh"], ["orow"], cp(T.orow[:, 0:C].indirect(T[own][:, 0:KB]), T.fh[:]))
         if t == 0:
-            later_constants()
-        do("s", ["orow", land], ["j0"], act(T.j0[:], T.orow[:, 0:C].indirect(T[land][:, 0:KB])))
-        shifted("j0", "b0", 1.0 / 1024)
-        h = wrap(T.j0[:], "j0")
-        do("v", ["hrow"], ["off0"], ts(T.off0[:], h, float(LIFT + HALF), A.add))
-        win, wkey = T.j0, "j0"
+            do("s", ["fh"], ["thr"], act(T.thr[:], T.fh[:], F.Identity, bias=-0.5))
+            do("s", ["ctl"], ["ctlp"], act(T.ctlp[:], T.ctl[:], scale=1.0 / 1024))
+        m, e, d = 16 * HIGH, LOW // 16, 1.0 / 1024
+        do("s", ["orow", land + ":h"], ["j0:h"], act(T.j0[:, m:C], T.orow[:, 0:C].indirect(T[land][:, HIGH:KB])))
+        bkeys = [shift("s", "j0", ["j0:h"], "b0", d, m, C)]
+        while later:
+            later.pop(0)()
+        h = wrap(T.j0, ["j0:h"], (m, C), to=["hrow:h"])
+        do("v", ["hrow:h"], ["off0:h"], ts(T.off0[:, HIGH:KB], h, float(LIFT + HALF), A.add))
+        do("s", ["orow", land + ":l"], ["j0:s"], act(T.j0[:, 0:LOW], T.orow[:, 0:C].indirect(T[land][:, 0:e])))
+        do("v", ["orow", land + ":l"], ["j0:v"], cp(T.j0[:, LOW:m], T.orow[:, 0:C].indirect(T[land][:, e:HIGH])))
+        h = wrap(T.j0, ["j0:s", "j0:v"], (0, m), to=["hrow:l"])
+        bkeys.append(shift("v", "j0", ["j0:v"], "b0", d, LOW, m))
+        do("v", ["hrow:l"], ["off0:l"], ts(T.off0[:, 0:HIGH], h, float(LIFT + HALF), A.add))
+        bkeys.append(shift("v", "j0", ["j0:s"], "b0", d, 0, LOW))
+        win, wkeys = T.j0, three("j0")
         for k in range(9):
             off, j, jn = "off%d" % (k % 2), "j%d" % (k % 2), "j%d" % ((k + 1) % 2)
             an, bk, bn = "a%d" % (k % 2), "b%d" % (k % 2), "b%d" % ((k + 1) % 2)
             if k < 8:
-                do("s", [j, off], [jn], act(T[jn][:], T[j][:, 0:C].indirect(T[off][:, 0:KB])))
-            do("v", [wkey, off, bk + ":s", bk + ":v"], [an], tt(T[an][:], win[:, 0:C].indirect(T[off][:, 0:KB]), T[bk][:], A.min))
-            win, wkey = T[an], an
+                do("s", three(j) + both(off), three(jn), act(T[jn][:], T[j][:, 0:C].indirect(T[off][:, 0:KB])))
+            do("v", wkeys + both(off) + bkeys, [an], tt(T[an][:], win[:, 0:C].indirect(T[off][:, 0:KB]), T[bk][:], A.min))
+            for key in bkeys:
+                reader.setdefault(bk + "*", []).extend(reader.get(key, []))
+            win, wkeys = T[an], [an]
             if k < 8:
-                shifted(an, bn, (2.0 ** (k + 1)) / 1024)
-                h = wrap(T[jn][:], jn)
+                d = (2.0 ** (k + 1)) / 1024
+                for q in "sv":
+                    before(q, [], [bn + "*"])
+                reader[bn + "*"] = []
+                bkeys = [shift("s", an, [an], bn, d, 0, CUT[0])]
+                h = wrap(T[jn], three(jn))
+                bkeys.append(shift("v", an, [an], bn, d, CUT[0], CUT[1]))
                 o = "off%d" % ((k + 1) % 2)
-                do("v", ["hrow"], [o], ts(T[o][:], h, float(LIFT + HALF), A.add))
-        do("v", [wkey, "ctl"], ["hkey"], scan(T.hkey[:], win[:], T.ctl[:], -1024.0, A.max, A.add))
+                do("v", both("hrow"), both(o), ts(T[o][:], h, float(LIFT + HALF), A.add))
+                bkeys.append(shift("v", an, [an], bn, d, CUT[1], C))
+        wkey = wkeys[0]
         do("v", [wkey, "thr"], ["wrow"], scan(T.wrow[:], win[:], T.thr[:], -1024.0, A.max, A.max))
-        do("v", ["hkey"], ["offm"], ts(T.offm[:], T.hkey[:, 15:C:16], float(MAGIC + LIFT + HALF), A.add, float(MAGIC), A.subtract))
-        do("v", ["wrow", "thr1"], ["crow"], scan(T.crow[:], T.wrow[:], T.thr1[:], -HALF - 1.5 - HALF / 1024, A.add, A.subtract))
-        do("v", ["crow", "offm", wkey], ["prow"], tt(T.prow[:], T.crow[:, 0:C].indirect(T.offm[:, 0:KB]), win[:], A.subtract))
-        h = wrap(T.prow[:], "prow", "ctlp")
-        do("v", ["hrow"], ["offp"], ts(T.offp[:], h, (LIFT + HALF) / 1024, A.add, 1024.0, A.mult))
+        do("v", [wkey, "ctl"], ["hkey"], scan(T.hkey[:], win[:], T.ctl[:], -1024.0, A.max, A.add))
+        do("v", ["wrow", "thr"], ["crow"], scan(T.crow[:], T.wrow[:], T.thr[:], -HALF / 1024, A.add, A.subtract))
+        own_key, up = T.hkey[:, 15:C:16], float(MAGIC + LIFT + HALF)
+        do("v", ["hkey"], ["offm"], ts(T.offm[:], own_key, up, A.add, float(MAGIC), A.subtract))
+        do("v", ["hkey"], ["mw"], ts(T.mw[:], own_key, up, A.add, float(MAGIC), A.subtract))
+        for q, a, b in (("s", 0, ENDS), ("v", ENDS, C)):
+            src = T.crow[:, 0:C].indirect(T.offm[:, a // 16:b // 16])
+            do(q, ["crow", "offm"], ["prow:" + q], act(T.prow[:, a:b], src) if q == "s" else cp(T.prow[:, a:b], src))
+        do("v", ["hkey", "mw"], ["kw"], tt(T.kw[:], own_key, T.mw[:], A.subtract))
+        h = wrap(T.prow, ["prow:s", "prow:v"], ctl="ctlp")
+        do("v", both("hrow") + ["kw"], ["pw"], tt(T.pw[:], h, T.kw[:], A.subtract))
+        do("v", ["pw"], ["offp"], ts(T.offp[:], T.pw[:], (LIFT + HALF) / 1024 - LIFT - HALF - 0.5, A.add, 1024.0, A.mult))
         do("v", ["offp", "fh"], ["erow"], cp(T.erow[:, 0:C].indirect(T.offp[:, 0:KB]), T.fh[:]))
-        h = wrap(T.erow[:], "erow")
+        h = wrap(T.erow, ["erow"])
         for i in (2, 0, 3, 1):
-            do("v", ["hrow"], ["offe%d" % i], ts(T["offe%d" % i][:], h, LIFT + HALF + 0.25 * i, A.add, 4.0, A.mult))
+            do("v", both("hrow"), ["offe%d" % i], ts(T["offe%d" % i][:], h, LIFT + HALF + 0.25 * i, A.add, 4.0, A.mult))
 
     def lay_out(t, tile, key, part):
         a, b = part
@@ -411,13 +444,13 @@ def rank_program(g, core, T, topo):
                 bank = ("pr%d" if h == 1 else "pp%d") % i
                 do("v", [bank, "z64:%d" % i], ["r%d:%d" % (i, h)],
                    tt(T["r%d" % i][:, a:b], T[bank][:, 0:b - a], T.z64[:, 4 * a + i:4 * b:4], A.add))
-        a, b = H1
-        for i in range(4):
-            do("s", ["r%d:%d" % (i, h) for h in HALVES], ["x%d:1:%d" % (t + 1, i)], act(xn[:, 4 * a + i:4 * b:4], T["r%d" % i][:, a:b], scale=0.015625))
+        for h, (a, b) in HALVES.items():
+            for i in range(4):
+                do("s", ["r%d:%d" % (i, h)], ["x%d:%d:%d" % (t + 1, h, i)], act(xn[:, 4 * a + i:4 * b:4], T["r%d" % i][:, a:b], scale=0.015625))
 
     def unpack(t, i, start, stop):
         qc, sc = "qc%d" % t, "sc%d" % t
-        matmul(T["pr%d" % i][:, 0:S], "pr%d" % i, T.qe[:, S * i:S * i + S], T.se[:, S * i:S * i + S], ["qe"], T[qc][:], T[sc][:], [qc, sc], start, stop)
+        matmul(T["pr%d" % i][:, 0:S], "pr%d" % i, T.qe[:, S * i:S * i + S], T.se[:, S * i:S * i + S], ["qe%d" % i], T[qc][:], T[sc][:], [qc, sc], start, stop)
 
     def arrive(t):
         zt, qz, sz = T["zt%d" % t], T["qz%d" % t], T["sz%d" % t]
@@ -454,6 +487,7 @@ def rank_program(g, core, T, topo):
     score(0, 1, H1)
     quant_state(0, 2, H2)
     score(0, 2, H2)
+    do("v", ["gs"], ["qg"], quant(T.qg[:], T.sg[:], T.gs[:]))
     take_scores(0, 1, H1)
     take_scores(0, 2, H2)
     for t in range(R):
@@ -462,7 +496,7 @@ def rank_program(g, core, T, topo):
         bt, qb, sb, qc, sc = ["%s%d" % (n, t) for n in ("bt", "qb", "sb", "qc", "sc")]
         lay_out(t, T[bt], bt + ":", H2)
         do("v", [bt + ":%d" % i for i in range(4)], [qb, sb], quant(T[qb][:], T[sb][:], T[bt][:]))
-        send(t, [(qc, qb, lambda n: T[n][:].bitcast(dt.uint8), qb), (sc, sb, lambda n: T[n][:], sb)], "rxb%d" % t)
+        send(t, [(qc, qc, qb, lambda n: T[n][:].bitcast(dt.uint8), qb), (sc, sc, sb, lambda n: T[n][:], sb)], "rxb%d" % t)
         stay(t)
         if t == R - 1:
             do("s", ["erow"], ["elf"], act(T.elf[:], T.erow[:], F.Identity, bias=float(HALF)))

from concourse.mybir import dt, AluOpType as A, ActivationFunctionType as F

C, S, R = 448, 128, 2
STEP = [1, 2]
KB = C // 16
NQ = KB // 4
WIDE = [max(128, 64 * (i + 1)) for i in range(NQ)]
AT = [sum(WIDE[:i]) for i in range(NQ + 1)]
BY_S = [27, 26, 25, 24, 7, 22, 21, 11, 10, 9, 8]
FIRST = 24
HIGH = 12
PLAN = [*range(20, 12, -1), 6, 12, "q6", "q3", 23, 5, "q4", "early", 4, 3, 2, "q5", 1, 0, "q1", "tallyh", "c", "q2", "high", "q0",
        "tallyl", "c"]
BY_V = sorted(k for k in PLAN if k in range(KB))
ENGINES = 8
H2, H1 = (0, S), (S, C)
HALVES = {1: (S, S + 160), 3: (S + 160, C)}
HALF = C // 2
LIFT = 480
DEEP = 1024
CUT = (320, 384)
LOW = 96
ENDS = 224
MAGIC = 12582912

SCRATCH = {}


def _buf(dtype, n, *names):
    for name in names:
        SCRATCH[name] = ("psum" if name[:2] in ("pp", "pr") and name[2:].isdigit() else "sbuf", [128, n], dtype)


_buf("bfloat16", 512, "ub", "vb", "neg", "c64", "go", "gs", "bt0", "bt1")
_buf("bfloat16", 4 * 512, "eb")
_buf("bfloat16", C, "mask", "gate", "ctl", "ctlp", "fh", "orow", "crow", "prow", "erow", "j0", "j1",
     "eqr", "eqs", "rel0", "rel1", "rel2", "rel3")
_buf("float16", C, "hrow")
_buf("bfloat16", 224 * KB, "zs")
_buf("bfloat16", 4 * C, "z64", "x0", "x1", "x2", "zt0", "zt1")
_buf("float8_e4m3fn_x4", 128, "qu", "qur", "qv", "qg", "qb0", "qb1", "qc0", "qc1")
_buf("uint8", 128, "su", "sur", "sv", "sg", "sb0", "sb1", "sc0", "sc1")
_buf("float8_e4m3fn_x4", 512, "qw", "qe")
_buf("uint8", 512, "sw", "se")
_buf("float8_e4m3fn_x4", C, "qx0", "qx1", "qx2", "qz0", "qz1")
_buf("uint8", C, "sx0", "sx1", "sx2", "sz0", "sz1")
_buf("bfloat16", 4 * AT[NQ], "fl")
_buf("float8_e4m3fn_x4", AT[NQ], "qf")
_buf("uint8", AT[NQ], "sf")
_buf("int32", C, "ci", "d15")
_buf("int32", 8, "ku")
_buf("uint16", 8, "offu")
_buf("uint16", KB, "offm", "offp", "off0", "off1", "own0", "own1", "land0", "land1", "offe0", "offe1", "offe2", "offe3")
_buf("float32", C, "thr", "mrow", "arow", "srow", "ctlb", "hkey", "hcol", "wrow", "elf", "ysb",
     "a0", "a1", "b0", "b1", "r0", "r1", "r2", "r3")
_buf("float32", KB, "k0", "k1", "cnt", "tie", "la", "lb", "lc", "mw", "kw", "pw")
_buf("float32", 32, "aw")
_buf("float32", 512, "pp0", "pp1", "pp2", "pp3", "pr0", "pr1", "pr2", "pr3")

LOADS = ["ldu", "ldx1", "ldx2", "ldw", "ldv"]
SEMAPHORES = ["cv", "cs", "ct", "cg", "stored", "sent", "rxh0", "rxh1", "rxl0", "rxl1", "rxb0", "rxb1"] + LOADS


def rank_program(g, core, T, topo):
    rank = T.rank_of(core)
    if rank is None:
        return
    queue = {"v": g.vector, "s": g.scalar, "t": g.tensor, "g": g, "y": g.sync}
    count = {}
    know = {q: {} for q in queue}
    writer, reader = {}, {}

    def wait(q, tok):
        _, sem, val, seen = tok
        if know[q].get(sem, 0) >= val:
            return
        queue[q].wait_ge(T.sem[sem], val)
        for s, n in list(seen.items()) + [(sem, val)]:
            know[q][s] = max(know[q].get(s, 0), n)

    def before(q, reads, writes):
        for k in reads:
            for tok in writer.get(k, []):
                wait(q, tok)
            if k[:2] in ("pp", "pr"):
                for tok in reader.get(k, []):
                    if tok[0] != q:
                        wait(q, tok)
        for k in writes:
            for tok in writer.get(k, []) + reader.get(k, []):
                wait(q, tok)

    def after(q, sem, inc, reads, writes):
        count[sem] = count.get(sem, 0) + inc
        tok = (q, sem, count[sem], dict(know[q]))
        for k in reads:
            reader.setdefault(k, []).append(tok)
        for k in writes:
            writer[k], reader[k] = [tok], []

    def do(q, reads, writes, make):
        before(q, reads, writes)
        make(queue[q]).then_inc(T.sem["c" + q], 1)
        after(q, "c" + q, 1, reads, writes)

    def load(q, sem, total, key, out, in_):
        queue[q].dma_start(out, in_).then_inc(T.sem[sem], 16)
        count[sem] = count.get(sem, 0) + 16
        writer.setdefault(key, []).append((q, sem, total, {}))

    def store(q, reads, out, in_):
        before(q, reads, [])
        queue[q].dma_start(out, in_).then_inc(T.sem["stored"], 16)
        after(q, "stored", 16, reads, [])

    def send(t, pairs, sem):
        dst = T.cores[rank ^ STEP[t]]
        rid, pid, _ = topo.addr(dst)
        eng = topo.engines(core, dst)[:ENGINES]
        mask = sum(1 << e for e in eng)
        total = count.get(sem, 0) + len(pairs) * len(eng)
        for land, there, here, view, key in pairs:
            before("g", [key], [])
            g.remote_dma(view(there), view(here), T.sem[sem], T.sem["sent"], pid, rid, mask)
            count["sent"] = count.get("sent", 0) + len(eng)
            writer[land] = [("far", sem, total, {})]
        count[sem] = total

    def ts(out, in0, s1, op0, s2=None, op1=None):
        if op1 is None:
            return lambda e: e.tensor_scalar(out, in0, s1, None, op0)
        return lambda e: e.tensor_scalar(out, in0, s1, s2, op0, op1)

    def tt(out, in0, in1, op):
        return lambda e: e.tensor_tensor(out, in0, in1, op)

    def act(out, in_, func=F.Copy, **kw):
        return lambda e: e.activation(out, in_, func, **kw)

    def cp(out, in_):
        return lambda e: e.tensor_copy(out, in_)

    def fill(out, x):
        return lambda e: e.memset(out, x)

    def quant(q, s, x):
        return lambda e: e.quantize_mx(q, s, x)

    def scan(out, d0, d1, init, op0, op1):
        return lambda e: e.tensor_tensor_scan(out, d0, d1, init, op0, op1)

    def back(a, b):
        return slice(b - 1, a - 1 if a else None, -1)

    def iota(name, pattern, base, cm, cols=slice(None), key=None):
        kw = {} if SCRATCH[name][2] == "int32" else {"allow_small_or_imprecise_dtypes": True}
        do("g", [], [key or name], lambda e: e.iota(T[name][:, cols], pattern, base, cm, **kw))

    load("s", "ldu", 16, "ub", T.ub[:], T.u[:])
    load("y", "ldx1", 16, "x0:1", T.x0[:, 4 * S:4 * C], T.x[:, 4 * S:4 * C])
    load("y", "ldx2", 16, "x0:2", T.x0[:, 0:4 * S], T.x[:, 0:4 * S])
    before("y", ["x0:1", "x0:2"], [])
    load("y", "ldw", 32, "w", T.qw[:].bitcast(dt.uint8), T.wc[:])
    load("y", "ldw", 32, "w", T.sw[:], T.ws[:])
    load("y", "ldv", 16, "vb", T.vb[:], T.v[:])

    iota("ci", [[-1, C]], C - 1, 1)
    iota("ku", [[16, 8]], 0, 0)
    do("v", [], ["neg"], fill(T.neg[:], -1.0))
    do("g", ["neg"], ["go"], lambda e: e.affine_select(T.go[:], T.neg[:], [[-16, 8], [0, 64]], A.is_ge, 0.0, 0, 1))
    do("g", ["go"], ["gs"], lambda e: e.affine_select(T.gs[:], T.go[:], [[16, 8], [0, 64]], A.is_ge, 0.0, 15, -1))
    left, k0_keys = [], []
    for k in range(KB):
        n = C - 16 * k - 16 * sum(i >= k for i in BY_S) - 1 - DEEP
        left.append(n + (16 * k if k in BY_S else HALF if k else 0))
    k = 0
    while k < KB:
        step, n = (left[k + 1] - left[k] if 0 < k < KB - 1 else 0), 1
        while 0 < k and k + n < KB and left[k + n] - left[k + n - 1] == step:
            n += 1
        k0_keys.append("k0:%d" % k)
        iota("k0", [[step, n]], left[k], 0, slice(k, k + n), k0_keys[-1])
        k += n
    do("v", [], ["c64"], fill(T.c64[:], 64.0))
    do("v", [], ["cnt0"], fill(T.cnt[:, 0:1], 0.0))
    do("v", ["ci"], ["d15"], ts(T.d15[:], T.ci[:], 15, A.bitwise_and))
    do("v", ["d15"], ["ctl"], ts(T.ctl[:], T.d15[:], 64.0, A.mult, -float(LIFT), A.add))
    own_q = T.d15[:, 15:C:16]
    do("v", ["d15"], ["la"], ts(T.la[:], own_q, -1.0, A.mult, 15.0, A.add))
    do("v", ["d15"], ["lb"], ts(T.lb[:], own_q, -32.0, A.mult, -32.0, A.add))
    do("v", ["ctl"], ["mask"], ts(T.mask[:], T.ctl[:], float(LIFT), A.is_equal))
    do("v", ["la", "lb"], ["lc"], tt(T.lc[:], T.la[:], T.lb[:], A.mult))
    do("v", ["ctl"], ["gate"], ts(T.gate[:], T.ctl[:], float(LIFT), A.not_equal))
    do("v", ["lc"], ["ctl"], ts(T.ctl[:, 15:C:16], T.lc[:], -float(LIFT), A.add))
    do("v", ["ku"], ["offu"], cp(T.offu[:], T.ku[:]))
    do("v", ["ub"], ["qu"], quant(T.qu[:], T.su[:], T.ub[:]))
    do("v", ["qu", "offu"], ["qur"], cp(T.qur[:, 0:128].bitcast(dt.uint32), T.qu[:, 0:128].bitcast(dt.uint32).indirect(T.offu[:, 0:8])))
    do("v", ["qu", "offu"], ["sur"], cp(T.sur[:, 0:128], T.su[:, 0:128].indirect(T.offu[:, 0:8])))
    for i in range(NQ):
        for j in range(64 * i, WIDE[i], 64):
            z = 4 * (AT[i] + j)
            do("s", ["neg"], ["fl%d" % k for k in range(4 * i, 4 * i + 4)] if j == 64 * i else ["flz%d" % i],
               act(T.fl[:, z:z + 256], T.neg[:, 0:256], scale=0.0))
    do("s", ["ctl"], ["ctlb"], act(T.ctlb[:], T.ctl[:]))
    iota("fh", [[1, C]], -HALF, 0)
    for b in range(4):
        do("g", ["c64"], ["eb%d" % b], lambda e: e.affine_select(
            T.eb[:, 512 * b:512 * b + 512], T.c64[:], [[-1, 512]], A.is_equal, 0.0, b, 4))

    def quant_const(b):
        do("v", ["eb%d" % b], ["qe%d" % b], quant(T.qe[:, S * b:S * b + S], T.se[:, S * b:S * b + S], T.eb[:, 512 * b:512 * b + 512]))

    later = [lambda b=b: quant_const(b) for b in range(4)] + [lambda: do("v", ["vb"], ["qv"], quant(T.qv[:], T.sv[:], T.vb[:]))]

    def matmul(out, key, lhs, ls, lkey, rhs, rs, rkey, start=True, stop=True):
        do("t", lkey + rkey, [key], lambda e: e.matmul_mx(out, lhs, ls, rhs, rs, start, stop))

    def state_keys(t, h):
        if t == 0:
            return ["x0:%d" % h]
        return ["x%d:%d:%d" % (t, c, i) for c in ((1, 3) if h == 1 else (2,)) for i in range(4)]

    def quant_state(t, h, part):
        a, b = part
        do("v", state_keys(t, h), ["qx%d:%d" % (t, h)], quant(T["qx%d" % t][:, a:b], T["sx%d" % t][:, a:b], T["x%d" % t][:, 4 * a:4 * b]))

    def score(t, h, part):
        a, b = part
        qx, sx = T["qx%d" % t], T["sx%d" % t]
        for p in ("pp0", "pp1") if h == 1 else ("pp2", "pp3"):
            matmul(T[p][:, 0:b - a], p, T.qur[:], T.sur[:], ["qur", "sur"], qx[:, a:b], sx[:, a:b], ["qx%d:%d" % (t, h)])

    def take_scores(t, h, part):
        a, b = part
        p0, p1 = ("pp0", "pp1") if h == 1 else ("pp2", "pp3")
        do("v", [p0, "mask"], ["mrow:%d" % h], tt(T.mrow[:, a:b], T[p0][:, 0:b - a], T.mask[:, a:b], A.mult))
        do("s", [p1], ["srow:%d" % h], act(T.srow[:, a:b], T[p1][:, 0:b - a]))
        do("v", ["mrow:%d" % h, "gate"], ["arow:%d" % h], scan(T.arow[:, back(a, b)], T.gate[:, back(a, b)], T.mrow[:, back(a, b)], 0.0, A.mult, A.add))

    def add_base(a, b):
        keys = ["cnt%d" % k if k in BY_S else "cntv%d" % (k >= HIGH) if k else "cnt0" for k in range(a, b)]
        do("v", keys + ["tie", "ctlb"], ["ctlb:%d" % a], tt(T.ctlb[:, 16 * a + 15:16 * b:16], T.cnt[:, a:b], T.tie[:, a:b], A.add))

    def settle(t, bank, a, b):
        do("v", [bank, "ctlb:%d" % a], ["hcol:%d" % a], scan(T.hcol[:, 16 * a:16 * b], T[bank][:, 16 * a:16 * b], T.ctlb[:, 16 * a:16 * b], -float(DEEP), A.max, A.add))
        key = "own%d:%d" % (t, a)
        do("v", ["hcol:%d" % a], [key], ts(T["own%d" % t][:, a:b], T.hcol[:, 16 * a + 15:16 * b:16], float(DEEP), A.add))
        h = "h" if a >= HIGH else "l"
        send(t, [("land%d:%s" % (t, h), "land%d" % t, "own%d" % t, lambda n: T[n][:, a:b], key)], "rx%s%d" % (h, t))

    def places(t):
        row = ["srow:1", "srow:2"]
        do("v", ["arow:1", "arow:2"], ["aw"], cp(T.aw[:, 0:KB], T.arow[:, 0:C:16]))
        pend, done = [], []

        def flags(k, a, b):
            z = 4 * AT[k // 4]
            return T.fl[:, z + 4 * a + k % 4:z + 4 * b:4]

        def sign(k):
            rel = "rel%d" % (k % 4)
            do("s", [rel], ["fl%d" % k, "cnt%d" % k], act(flags(k, 0, 16 * k), T[rel][:, 0:16 * k], F.Sign, scale=-1.0, accum_out=T.cnt[:, k:k + 1]))
            do("s", [rel], ["fld%d" % k], act(flags(k, 16 * k, 16 * k + 16), T[rel][:, 16 * k:16 * k + 16], F.Sign, scale=-1.0))

        for k in BY_S:
            rel = "rel%d" % (k % 4)
            do("s", row + ["aw"], [rel], act(T[rel][:, 0:16 * k + 16], T.srow[:, 0:16 * k + 16], F.Relu, bias=T.aw[:, k:k + 1], scale=-1.0))
            pend.append(k)
            if len(pend) > 1:
                sign(pend.pop(0))
        sign(pend.pop(0))

        def add_up(k):
            z = 224 * k + 224
            do("v", ["fl%d" % k], ["zs:%d" % k], scan(T.zs[:, z - 8 * k:z], flags(k, 0, 8 * k), flags(k, 8 * k, 16 * k), -float(HALF), A.add, A.add))

        def tally(a, b, n):
            ks = [k for k in BY_V if a <= k < b]
            at, runs = 0, []
            while at < len(ks):
                end = at
                while end + 1 < len(ks) and ks[end + 1] == ks[end] + 1:
                    end += 1
                runs.append((ks[at], ks[end] + 1))
                at = end + 1
            for i, (c, d) in enumerate(runs):
                key = "cntv%d" % n
                do("v", ["zs:%d" % k for k in range(c, d)], [key] if i == len(runs) - 1 else [key + "'"],
                   cp(T.cnt[:, c:d], T.zs[:, 224 * c + 223:224 * d:224]))

        def sum_up(i):
            a, b = AT[i], AT[i + 1]
            keys = [n % k for k in range(4 * i, 4 * i + 4) for n in ("fl%d", "fld%d")] + ["flz%d" % i]
            do("v", keys, ["qf%d" % i], quant(T.qf[:, a:b], T.sf[:, a:b], T.fl[:, 4 * a:4 * b]))

            def add(bank, n, start, stop):
                matmul(T[bank][:, 0:n], bank, T.qg[:], T.sg[:], ["qg"], T.qf[:, a:a + n], T.sf[:, a:a + n], ["qf%d" % i], start, stop)
            last = len([j for j in done if j >= HIGH // 4]) == NQ - HIGH // 4 - 1
            if i >= HIGH // 4:
                if t == 0 and i == NQ - 1:
                    add("pp3", C, True, True)
                add("pp1", b - a, not any(j >= HIGH // 4 for j in done), last)
            add("pp2", min(16 * HIGH, b - a), not done, len(done) == NQ - 1)
            done.append(i)

        prev, n = None, 0
        for step in PLAN:
            if step == "c":
                for _ in range(2 if t == 0 else 0):
                    later.pop(0)()
            elif step == "early":
                if t == 0:
                    add_base(FIRST, KB)
                    settle(t, "pp3", FIRST, KB)
            elif step == "tallyh":
                tally(HIGH, KB, 1)
                add_base(HIGH, FIRST if t == 0 else KB)
            elif step == "high":
                settle(t, "pp1", HIGH, FIRST if t == 0 else KB)
            elif step == "tallyl":
                tally(1, HIGH, 0)
                add_base(0, HIGH)
            elif step in ["q%d" % i for i in range(NQ)]:
                sum_up(int(step[1]))
            else:
                k = step
                do("v", row + ["aw"], ["fl%d" % k], ts(flags(k, 0, 16 * k + 16), T.srow[:, 0:16 * k + 16], T.aw[:, k:k + 1], A.is_ge))
                if prev:
                    add_up(prev)
                prev = k
                n += 1
                if n == 1:
                    for h, p, (a, b) in ((1, "pp0", H1), (2, "pp2", H2)):
                        do("v", ["arow:%d" % h, p], ["eqr:%d" % h], tt(T.eqr[:, a:b], T.arow[:, a:b], T[p][:, 0:b - a], A.is_equal))
                if n == 2:
                    do("v", ["eqr:1", "eqr:2", "gate"], ["eqs"], scan(T.eqs[:, back(0, C)], T.gate[:, back(0, C)], T.eqr[:, back(0, C)], 0.0, A.mult, A.add))
                    if t == 0:
                        do("v", ["lc"] + k0_keys, ["k1"], tt(T.k1[:], T.lc[:], T.k0[:], A.add))
                if n == 3:
                    do("v", ["eqs", "k1"], ["tie"], tt(T.tie[:], T.eqs[:, 0:C:16], T.k1[:], A.add))
        settle(t, "pp2", 0, HIGH)

    def wrap(row, keys, part=(0, C), ctl="ctl", to=("hrow:l", "hrow:h")):
        a, b = part
        do("v", keys + [ctl], list(to), scan(T.hrow[:, a:b], row[:, a:b], T[ctl][:, a:b], -1024.0, A.max, A.add))
        return T.hrow[:, a + 15:b:16]

    def three(name):
        return [name + ":s", name + ":v", name + ":h"]

    def both(name):
        return [name + ":l", name + ":h"]

    def shift(q, an, keys, bn, d, a, b):
        do(q, keys, [bn + ":%d" % a], act(T[bn][:, a:b], T[an][:, a:b], F.Identity, bias=-d) if q == "s"
           else ts(T[bn][:, a:b], T[an][:, a:b], -d, A.add))
        return bn + ":%d" % a

    def cycles(t):
        own, land = "own%d" % t, "land%d" % t
        parts = [own + ":0", own + ":%d" % HIGH] + ([own + ":%d" % FIRST] if t == 0 else [])
        do("v", parts + ["fh"], ["orow"], cp(T.orow[:, 0:C].indirect(T[own][:, 0:KB]), T.fh[:]))
        if t == 0:
            do("s", ["fh"], ["thr"], act(T.thr[:], T.fh[:], F.Identity, bias=-0.5))
            do("s", ["ctl"], ["ctlp"], act(T.ctlp[:], T.ctl[:], scale=1.0 / 1024))
        m, e, d = 16 * HIGH, LOW // 16, 1.0 / 1024
        do("s", ["orow", land + ":h"], ["j0:h"], act(T.j0[:, m:C], T.orow[:, 0:C].indirect(T[land][:, HIGH:KB])))
        bkeys = [shift("s", "j0", ["j0:h"], "b0", d, m, C)]
        while later:
            later.pop(0)()
        h = wrap(T.j0, ["j0:h"], (m, C), to=["hrow:h"])
        do("v", ["hrow:h"], ["off0:h"], ts(T.off0[:, HIGH:KB], h, float(LIFT + HALF), A.add))
        do("s", ["orow", land + ":l"], ["j0:s"], act(T.j0[:, 0:LOW], T.orow[:, 0:C].indirect(T[land][:, 0:e])))
        do("v", ["orow", land + ":l"], ["j0:v"], cp(T.j0[:, LOW:m], T.orow[:, 0:C].indirect(T[land][:, e:HIGH])))
        h = wrap(T.j0, ["j0:s", "j0:v"], (0, m), to=["hrow:l"])
        bkeys.append(shift("v", "j0", ["j0:v"], "b0", d, LOW, m))
        do("v", ["hrow:l"], ["off0:l"], ts(T.off0[:, 0:HIGH], h, float(LIFT + HALF), A.add))
        bkeys.append(shift("v", "j0", ["j0:s"], "b0", d, 0, LOW))
        win, wkeys = T.j0, three("j0")
        for k in range(9):
            off, j, jn = "off%d" % (k % 2), "j%d" % (k % 2), "j%d" % ((k + 1) % 2)
            an, bk, bn = "a%d" % (k % 2), "b%d" % (k % 2), "b%d" % ((k + 1) % 2)
            if k < 8:
                do("s", three(j) + both(off), three(jn), act(T[jn][:], T[j][:, 0:C].indirect(T[off][:, 0:KB])))
            do("v", wkeys + both(off) + bkeys, [an], tt(T[an][:], win[:, 0:C].indirect(T[off][:, 0:KB]), T[bk][:], A.min))
            for key in bkeys:
                reader.setdefault(bk + "*", []).extend(reader.get(key, []))
            win, wkeys = T[an], [an]
            if k < 8:
                d = (2.0 ** (k + 1)) / 1024
                for q in "sv":
                    before(q, [], [bn + "*"])
                reader[bn + "*"] = []
                bkeys = [shift("s", an, [an], bn, d, 0, CUT[0])]
                h = wrap(T[jn], three(jn))
                bkeys.append(shift("v", an, [an], bn, d, CUT[0], CUT[1]))
                o = "off%d" % ((k + 1) % 2)
                do("v", both("hrow"), both(o), ts(T[o][:], h, float(LIFT + HALF), A.add))
                bkeys.append(shift("v", an, [an], bn, d, CUT[1], C))
        wkey = wkeys[0]
        do("v", [wkey, "thr"], ["wrow"], scan(T.wrow[:], win[:], T.thr[:], -1024.0, A.max, A.max))
        do("v", [wkey, "ctl"], ["hkey"], scan(T.hkey[:], win[:], T.ctl[:], -1024.0, A.max, A.add))
        do("v", ["wrow", "thr"], ["crow"], scan(T.crow[:], T.wrow[:], T.thr[:], -HALF / 1024, A.add, A.subtract))
        own_key, up = T.hkey[:, 15:C:16], float(MAGIC + LIFT + HALF)
        do("v", ["hkey"], ["offm"], ts(T.offm[:], own_key, up, A.add, float(MAGIC), A.subtract))
        do("v", ["hkey"], ["mw"], ts(T.mw[:], own_key, up, A.add, float(MAGIC), A.subtract))
        for q, a, b in (("s", 0, ENDS), ("v", ENDS, C)):
            src = T.crow[:, 0:C].indirect(T.offm[:, a // 16:b // 16])
            do(q, ["crow", "offm"], ["prow:" + q], act(T.prow[:, a:b], src) if q == "s" else cp(T.prow[:, a:b], src))
        do("v", ["hkey", "mw"], ["kw"], tt(T.kw[:], own_key, T.mw[:], A.subtract))
        h = wrap(T.prow, ["prow:s", "prow:v"], ctl="ctlp")
        do("v", both("hrow") + ["kw"], ["pw"], tt(T.pw[:], h, T.kw[:], A.subtract))
        do("v", ["pw"], ["offp"], ts(T.offp[:], T.pw[:], (LIFT + HALF) / 1024 - LIFT - HALF - 0.5, A.add, 1024.0, A.mult))
        do("v", ["offp", "fh"], ["erow"], cp(T.erow[:, 0:C].indirect(T.offp[:, 0:KB]), T.fh[:]))
        h = wrap(T.erow, ["erow"])
        for i in (2, 0, 3, 1):
            do("v", both("hrow"), ["offe%d" % i], ts(T["offe%d" % i][:], h, LIFT + HALF + 0.25 * i, A.add, 4.0, A.mult))

    def lay_out(t, tile, key, part):
        a, b = part
        for i in (2, 0, 3, 1):
            out = tile[:, 4 * a + i:4 * b:4]
            src = T["x%d" % t][:, 0:4 * C].indirect(T["offe%d" % i][:, a // 16:b // 16])
            do("v" if i < 2 else "s", state_keys(t, 1) + state_keys(t, 2) + ["offe%d" % i], [key + str(i)], cp(out, src) if i < 2 else act(out, src))

    def layer(t, i, qz, sz, a, b, key, bank, start=True):
        matmul(T[bank][:, 0:b - a], bank, T.qw[:, S * i:S * i + S], T.sw[:, S * i:S * i + S], ["w"], qz[:, a:b], sz[:, a:b], [key], start, True)

    def stay(t):
        zt, qz, sz, xn = T["zt%d" % t], T["qz%d" % t], T["sz%d" % t], T["x%d" % (t + 1)]
        for h, (a, b) in HALVES.items():
            zk = "z%d:%d:" % (t, h)
            lay_out(t, zt, zk, (a, b))
            do("v", [zk + str(i) for i in range(4)], ["qz%d:%d" % (t, h)], quant(qz[:, a:b], sz[:, a:b], zt[:, 4 * a:4 * b]))
            for i in range(4):
                layer(t, i, qz, sz, a, b, "qz%d:%d" % (t, h), ("pr%d" if h == 1 else "pp%d") % i)
        a, b = H1
        for i in range(4):
            out, src = T.z64[:, 4 * a + i:4 * b:4], zt[:, 4 * a + i:4 * b:4]
            reads = ["z%d:%d:%d" % (t, h, i) for h in HALVES]
            do("v" if i % 2 else "s", reads, ["z64:%d" % i], ts(out, src, 64.0, A.mult) if i % 2 else act(out, src, scale=64.0))
        for h, (a, b) in HALVES.items():
            for i in range(4):
                bank = ("pr%d" if h == 1 else "pp%d") % i
                do("v", [bank, "z64:%d" % i], ["r%d:%d" % (i, h)],
                   tt(T["r%d" % i][:, a:b], T[bank][:, 0:b - a], T.z64[:, 4 * a + i:4 * b:4], A.add))
        for h, (a, b) in HALVES.items():
            for i in range(4):
                do("s", ["r%d:%d" % (i, h)], ["x%d:%d:%d" % (t + 1, h, i)], act(xn[:, 4 * a + i:4 * b:4], T["r%d" % i][:, a:b], scale=0.015625))

    def unpack(t, i, start, stop):
        qc, sc = "qc%d" % t, "sc%d" % t
        matmul(T["pr%d" % i][:, 0:S], "pr%d" % i, T.qe[:, S * i:S * i + S], T.se[:, S * i:S * i + S], ["qe%d" % i], T[qc][:], T[sc][:], [qc, sc], start, stop)

    def arrive(t):
        zt, qz, sz = T["zt%d" % t], T["qz%d" % t], T["sz%d" % t]
        for i in range(4):
            unpack(t, i, True, True)
            do("v", ["pr%d" % i], ["z%d:2:%d" % (t, i)], ts(zt[:, i:4 * S:4], T["pr%d" % i][:, 0:S], 0.015625, A.mult))
        do("v", ["z%d:2:%d" % (t, i) for i in range(4)], ["qz%d:2" % t], quant(qz[:, 0:S], sz[:, 0:S], zt[:, 0:4 * S]))
        for i in range(4):
            unpack(t, i, True, False)
        for i in range(4):
            layer(t, i, qz, sz, 0, S, "qz%d:2" % t, "pr%d" % i, False)

    def arrived(t):
        for i in range(4):
            out, src = T["x%d" % (t + 1)][:, i:4 * S:4], T["pr%d" % i][:, 0:S]
            do("s" if i < 2 else "v", ["pr%d" % i], ["x%d:2:%d" % (t + 1, i)],
               act(out, src, scale=0.015625) if i < 2 else ts(out, src, 0.015625, A.mult))

    def finish(t, h, part):
        a, b = part
        q, s, key, p = T["qx%d" % t], T["sx%d" % t], "qx%d:%d" % (t, h), "pp0" if h == 1 else "pp2"
        store("y", [key], T.oc[:, 4 * a:4 * b], q[:, a:b].bitcast(dt.uint8))
        matmul(T[p][:, 0:b - a], p, T.qv[:], T.sv[:], ["qv"], q[:, a:b], s[:, a:b], [key])

    def store_rest(t, h, part):
        a, b = part
        s, key, p = T["sx%d" % t], "qx%d:%d" % (t, h), "pp0" if h == 1 else "pp2"
        do("s", [p], ["ysb:%d" % h], act(T.ysb[:, a:b], T[p][:, 0:b - a]))
        store("s", ["ysb:%d" % h], T.y[:, a:b], T.ysb[:, a:b])
        for k in range(4):
            store("y", [key], T.osc[4 * k:4 * k + 4, a:b], s[32 * k:32 * k + 4, a:b])

    quant_state(0, 1, H1)
    score(0, 1, H1)
    quant_state(0, 2, H2)
    score(0, 2, H2)
    do("v", ["gs"], ["qg"], quant(T.qg[:], T.sg[:], T.gs[:]))
    take_scores(0, 1, H1)
    take_scores(0, 2, H2)
    for t in range(R):
        places(t)
        cycles(t)
        bt, qb, sb, qc, sc = ["%s%d" % (n, t) for n in ("bt", "qb", "sb", "qc", "sc")]
        lay_out(t, T[bt], bt + ":", H2)
        do("v", [bt + ":%d" % i for i in range(4)], [qb, sb], quant(T[qb][:], T[sb][:], T[bt][:]))
        send(t, [(qc, qc, qb, lambda n: T[n][:].bitcast(dt.uint8), qb), (sc, sc, sb, lambda n: T[n][:], sb)], "rxb%d" % t)
        stay(t)
        if t == R - 1:
            do("s", ["erow"], ["elf"], act(T.elf[:], T.erow[:], F.Identity, bias=float(HALF)))
            store("y", ["elf"], T.el[:], T.elf[0:128:16, :])
        arrive(t)
        quant_state(t + 1, 1, H1)
        arrived(t)
        last, then = (score, take_scores) if t < R - 1 else (finish, store_rest)
        last(t + 1, 1, H1)
        quant_state(t + 1, 2, H2)
        last(t + 1, 2, H2)
        then(t + 1, 1, H1)
        then(t + 1, 2, H2)
    for sem in sorted(count):
        g.wait_ge(T.sem[sem], count[sem])
